import numpy as np, ml_dtypes
CORES = [35,38,43,46]
N = 4
BF = ml_dtypes.bfloat16
def gentries(a):
    return np.ascontiguousarray(a.reshape(8, 16, -1).transpose(0, 2, 1)).reshape(8, -1)
def gtable(e):
    e = np.asarray(e); return np.ascontiguousarray(e.reshape(8, -1, 16).transpose(0, 2, 1)).reshape(128, -1).astype(np.int32)
V, E, G, K, A, S, R = 2880, 64, 1536, 256, 32, 5, 448
W = V + (N - 1) * E
def far(d, g):
    return (g, 7 - g, (8 - g) % 8)[d % 3]
def watch(rng, ins, nd, out, dens):
    co = np.full((16, W), -1)
    for i in range(16):
        o = rng.permutation(G)[:int(dens * G)]
        j = (rng.random(len(o)) * np.maximum(nd[o], 1)).astype(np.int64)
        c = np.where(nd[o] > 0, ins[j, o], out[rng.integers(0, G, len(o))])
        c, first = np.unique(c, return_index=True); co[i, c] = o[first]
    return co
def lively(rng, dens=None, pa=None, sk=1.5, p=None):
    if dens is None: dens = rng.choice(np.array([0.12, 0.2, 0.3]))
    if pa is None: pa = rng.choice(np.array([0.15, 0.4, 0.65, 0.9]))
    if p is None: p = rng.permutation(V)
    al = rng.choice(np.array([0.06, 0.15, 0.3]))
    out, rest = p[:G].copy(), p[G:]; Z, B, T, U = rest[:R], rest[R:2 * R], rest[2 * R:2 * R + 24], rest[2 * R + 24:]
    x = np.full((16, V), -1); x[:, Z] = 0
    x[:, B] = (rng.random((16, R)) * (1 + rng.integers(1, 16, R))).astype(np.int64)
    x[:, T[:16]] = 15; x[rng.integers(0, 16, 8), T[8:16]] = 14; x[:, T[16:]] = 0; x[rng.integers(0, 16, 8), T[16:]] = 1
    kind = rng.choice(6, G, p=np.array([0.2, 0.33, 0.08, al, 0.06, 0.33 - al]))
    nd = np.where((kind == 1) | (kind == 2), rng.integers(1, 4, G), 0); nd = np.where(kind == 3, 1, nd); nd = np.where(kind == 4, rng.integers(2, 16, G), nd)
    zi = Z[rng.integers(0, R, (15, G))]
    ins = np.where((rng.random((15, G)) < 0.5) | (kind == 3) | (kind == 5), zi, B[rng.integers(0, R, (15, G))])
    h = rng.random((15, G)); ui = U[rng.integers(0, len(U), (15, G))]
    dep = np.where(h < 0.65, out[(G * rng.random((15, G)) ** sk).astype(np.int64)], np.where(h < 0.85, rng.integers(V, W, (15, G)), ui))
    dep = np.where((kind == 4) & (rng.random((15, G)) < 0.7), ui, dep)
    ins = np.where(np.arange(15)[:, None] < nd, dep, ins)
    ins[14] = np.where(kind == 2, T[rng.integers(0, 16, G)], ins[14])
    k5 = np.flatnonzero(kind == 5)
    if len(k5) == 0: k5 = np.arange(G)
    i3 = kind == 3
    ins[13] = np.where(i3 & (rng.random(G) < 0.2), out[k5[rng.integers(0, len(k5), G)]], ins[13])
    ins[12] = np.where(i3 & (rng.random(G) < 0.08), T[rng.integers(16, 24, G)], ins[12])
    ins[0] = np.where(i3 & (rng.random(G) < 0.04), out, ins[0])
    ins[1] = np.where(i3 & (rng.random(G) < 0.06), ins[0], ins[1])
    co = watch(rng, ins, nd, out, dens)
    gv = np.concatenate([np.take_along_axis(ins, np.argsort(rng.random((15, G)), axis=0), 0), out[None]])
    b = np.flatnonzero(rng.random(G) < 0.03); x[:, out[b]] = rng.integers(0, 16, (16, len(b)))
    return x, gv, co, (rng.random(G) < pa).astype(np.int64), out, Z, B, T, U
def alias(rng, q, k, u):
    k = np.asarray(k); q[1][:15, k] = q[5][rng.integers(0, R, (15, len(k)))]; q[1][rng.integers(0, 15, len(k)), k] = u; q[0][:, q[4][k]] = -1
def ready(rng, q, k):
    k = np.asarray(k); n = (15, len(k))
    q[1][:15, k] = np.where(rng.random(n) < 0.5, q[5][rng.integers(0, R, n)], q[6][rng.integers(0, R, n)]); q[0][:, q[4][k]] = -1
def exports(rng, P):
    n = (N - 1) * E
    return np.stack([np.stack([np.where(rng.random(n) < 0.75, q[4][(G * rng.random(n) ** 2).astype(np.int64)], rng.integers(0, V, n)) for q in p]) for p in P])
def pack(P, ex):
    def whole(i): return np.stack([np.concatenate([q[i] for q in p]) for p in P])
    return {"x0": whole(0).astype(np.float32).astype(BF), "gv": whole(1).astype(np.int32), "co": whole(2).astype(np.int32),
            "aw": np.stack([np.stack([q[3] for q in p]) for p in P]).astype(np.int32), "ex": np.stack([gtable(a) for a in ex])}
def setup_inputs(rng):
    P = [[lively(rng) for g in range(8)] for r in range(N)]
    return pack(P, exports(rng, P))
def setup_inputs_spread(rng):
    P = []
    for r in range(N):
        P.append([])
        for g in range(8):
            q = lively(rng, dens=rng.choice(np.array([0.03, 0.4, 0.9])), pa=rng.choice(np.array([0.05, 0.5, 1.0])), sk=4.0)
            s = np.flatnonzero(rng.random(G) < 0.2); q[1][:15, s] = rng.integers(0, W, (15, len(s)))
            q[0][:, q[6]] = np.minimum(np.exp2(4 * rng.random(R)) * rng.random((16, R)), 15).astype(np.int64)
            P[r].append(q)
    return pack(P, exports(rng, P))
def setup_inputs_ends(rng):
    P = []
    for r in range(N):
        P.append([])
        for g in range(8):
            p = np.insert(np.insert(1 + rng.permutation(V - 2), G - 1, V - 1), G, 0)
            q = lively(rng, p=p, pa=(0.15, 0.6)[(g // 2 + r) % 2]); x, gv, co, aw, out, Z, B, T, U = q
            x[:, B] = 15 * rng.integers(0, 2, (16, R))
            t = rng.integers(0, 7, G); ins = np.zeros((15, G), np.int64); own = out[(G * rng.random(G) ** 1.5).astype(np.int64)]
            ins[:4] = np.where(t == 0, B[rng.integers(0, R, (4, G))], 0)
            ins[0] = np.where((t == 1) | (t == 2), W - 1, np.where((t == 3) | (t == 5), own, ins[0]))
            ins[1] = np.where(t == 2, W - 1, np.where(t == 5, T[rng.integers(0, 16, G)], ins[1])); ins[2] = np.where(t == 2, W - 1, ins[2])
            ins = np.where(t == 4, W - 1, ins)
            co[:] = watch(rng, ins, ((t > 0) & (t < 6)).astype(np.int64), out, 0.2)
            gv[:15] = np.take_along_axis(ins, np.argsort(rng.random((15, G)), axis=0), 0)
            co[co == G - 1] = -1
            if g % 2: co[:, W - 1] = G - 1
            else: co[np.arange(16), out[:16]] = G - 1
            aw[0] = 1; aw[G - 1] = 1
            if (g + r) % 2: x[:, V - 1] = 15 * rng.integers(0, 2, 16)
            else:
                x[:, V - 1] = -1; gv[:15, G - 1] = 0; gv[:4, G - 1] = B[rng.integers(0, R, 4)]
            P[r].append(q)
    ex = exports(rng, P)
    ex = np.where(rng.random(ex.shape) < 0.75, np.where(rng.random(ex.shape) < 0.5, 0, V - 1), ex); ex[..., -1] = V - 1
    return pack(P, ex)
def setup_inputs_corners(rng):
    P = []
    for r in range(N):
        P.append([])
        for g in range(8):
            c = (g + 3 * r) % 8
            q = lively(rng, dens=0.9 if c == 7 else None); x, gv, co, aw, out, Z, B, T, U = q
            if c == 0: aw[:] = 0
            elif c == 1:
                aw[:] = 0; aw[G - 1] = 1; ready(rng, q, [G - 1]); hs = rng.permutation(G - 1)[:16]
                co[np.isin(co, hs)] = -1; co[np.arange(16), out[G - 1]] = hs
            elif c < 5:
                m, n = K + c - 3, A + c - 3; ix = np.sort(rng.permutation(G)[:m]); aw[:] = 0; aw[ix] = 1
                ready(rng, q, ix); k = ix[np.sort(rng.permutation(K - 1)[:n])]; u = U[rng.permutation(len(U))[:n]]
                alias(rng, q, k, u); co[:, u] = -1
            elif c == 5: aw[:] = 1
            elif c == 6:
                aw[:] = 1; co[:] = -1; n = min(S, G // K); j = np.arange(A)
                for t in range(n):
                    u = out[(t + 1) * K + j] if t + 1 < n else U[:A]
                    alias(rng, q, t * K + j, u); hs = rng.permutation(G); co[t, out[t * K + j]] = hs[:A]
                    if t + 1 < n: co[t, u[A - 1]] = hs[A]
            else:
                hs = rng.permutation(G)[:24]; aw[:12] = 1; alias(rng, q, np.arange(12), U[:12])
                co[np.isin(co, hs)] = -1; co[:, U[:12]] = -1; co[:, out[:12]] = -1
                for j in range(12):
                    a, b = ((16, 16), (0, 0), (8, 7 + j % 4 // 2))[j // 4]
                    co[:a, out[j]] = hs[j]; co[b:, U[j]] = hs[12 + j]
            P[r].append(q)
    return pack(P, exports(rng, P))
def setup_inputs_crowd(rng):
    P = []; k7 = np.arange(7, G, K)
    for r in range(N):
        P.append([])
        for g in range(8):
            c = (g + r) % 8; q = lively(rng); x, gv, co, aw, out, Z, B, T, U = q
            if c < 6: aw[:] = 1; co[:] = -1
            if c < 2:
                alias(rng, q, np.arange(G), np.full(G, U[0])); co[0, out[0]] = 5; co[0, out[K]] = 6
                if c == 0: alias(rng, q, [K - 1], [U[2]])
                if c == 1: alias(rng, q, k7, np.full(len(k7), U[1])); alias(rng, q, [3], [out[K - 1]])
            elif c < 4:
                gv[:15] = out[0]; x[:, out] = -1; ready(rng, q, [0]); co[np.arange(16), out[0]] = G - 1 - np.arange(16)
                if c == 3: gv[3, k7] = U[0]
            elif c < 6:
                ready(rng, q, np.arange(G))
                for i in range(16): co[i, out[:K]] = rng.permutation(G)[:K]
                co[co == G - 1] = -1; co[np.arange(16), out[:16]] = G - 1
                if c == 5: co[0, out[0]] = -1; gv[14, K - 1] = U[0]
            elif c == 7 and r < 2:
                hs = rng.permutation(G)[:(N - 1) * E]; ready(rng, q, hs); aw[:] = 0; co[:] = -1; co[0, V:] = hs
            P[r].append(q)
    ex = exports(rng, P)
    for r in range(1, N, 2):
        for g in range(8): ex[r, g] = P[r][g][4][0]
    for r in range(2):
        for d in range(1, N):
            g = far(d, 7 - r); ex[r ^ d, g, (d - 1) * E:d * E] = P[r ^ d][g][6][rng.integers(0, R, E)]
    g = far(1, 6); ex[0, g, 0] = P[0][g][8][2]
    return pack(P, ex)
def relay(rng, q):
    x, gv, co, aw, out, Z, B, T, U = q; co[:] = -1; aw[:] = 0; m = G - 1
    p = 1 + rng.permutation(G - 2); b = p[:S]; k, j, c, h, v = p[S:S + 5]
    ready(rng, q, b); gv[rng.integers(0, 15, S - 1), b[1:]] = out[b[:-1]]; co[0, out[b[:-1]]] = b[1:]
    alias(rng, q, [k, m, j, c, v], [out[m], U[0], U[0], U[1], out[b[S - 2]]])
    aw[[b[0], k, c]] = 1; co[1, out[b[S - 3]]] = m; co[1, out[b[S - 2]]] = k; co[2, out[b[S - 2]]] = j
    co[5, out[c]] = 0; co[5, U[1]] = h
    if S > 3: co[3, out[b[S - 4]]] = v
    else: aw[v] = 1
    return [(0, B[0]), (1, out[b[S - 1]]), (2, out[v])]
def quiet(rng, q, idle):
    x, gv, co, aw, out, Z, B, T, U = q; co[:] = -1; aw[:] = 0; y = rng.permutation(G)[:2]
    if idle:
        alias(rng, q, y, [V, V + 1]); aw[y] = 1
        return [(slice(E - 2, None, E), out[y[0]]), (2 * E, out[y[1]])]
    ready(rng, q, y[:1]); co[3, V + 2] = y[0]
    return []
def setup_inputs_calm(rng):
    P = []; put = []
    for r in range(N):
        P.append([])
        for g in range(8):
            odd = (g + r) % 2 == 1; end = odd and g > 5
            q = lively(rng, p=np.insert(1 + rng.permutation(V - 1), G + 2 * R + 24, 0) if end else None); P[r].append(q)
            if end: put += [(r, g, s, v) for s, v in relay(rng, q)]
            elif odd and g < 2: put += [(r, g, s, v) for s, v in quiet(rng, q, r // 2 % 2 == 0)]
            if odd: continue
            x, gv, co, aw, out, Z, B, T, U = q; n = (g // 2 + r) % 4
            co[:] = -1; aw[:] = 0; p = rng.permutation(G); b = p[:S]; a = p[S:4 * S].reshape(3, S); e = p[4 * S:7 * S].reshape(3, S); w = p[7 * S:7 * S + 3]
            ready(rng, q, b); aw[b[0]] = 1; gv[rng.integers(0, 15, S - 1), b[1:]] = out[b[:-1]]
            last = S if n else 3
            co[0, out[b[:last - 1]]] = b[1:last]
            for j in range(n):
                alias(rng, q, a[j], np.concatenate([out[a[j, 1:]], np.array([U[j] if j < 2 else W - 1])]))
                aw[a[j, 0]] = 1; co[1 + j, out[b[:-1]]] = a[j, 1:]; co[8 + np.arange(S), out[a[j]]] = w[j]
            if n == 3:
                for j in range(3):
                    ready(rng, q, e[j]); gv[0, e[j, 1:]] = out[b[:-1]]; gv[1:1 + j, e[j]] = U[10 + j]; co[4 + j, out[b[:-1]]] = e[j, 1:]
    ex = exports(rng, P)
    for r, g, s, v in put: ex[r, g, s] = v
    return pack(P, ex)
def check_inputs(d):
    bad = []
    for k, lo, hi in (("x0", -1, 15), ("gv", 0, W - 1), ("co", -1, G - 1), ("aw", 0, 1), ("ex", 0, V - 1)):
        v = np.asarray(d[k]).astype(np.float64)
        if not (np.min(v) >= lo and np.max(v) <= hi): bad.append("range of " + k)
    v = np.asarray(d["x0"]).astype(np.float32).reshape(N, 8, 16, V)
    if not np.all(v == np.floor(v)): bad.append("x0 holds whole numbers")
    if np.any(np.any(v < 0, axis=2) != np.all(v < 0, axis=2)): bad.append("a column of x0 is -1 on all rows of a group or on none")
    o = np.sort(np.asarray(d["gv"]).reshape(N, 8, 16, G)[:, :, 15], axis=-1)
    if np.min(o) < 0 or np.max(o) >= V: bad.append("range of the outputs in gv")
    if np.any(o[..., 1:] == o[..., :-1]): bad.append("outputs in gv differ")
    c = np.sort(np.asarray(d["co"]), axis=-1)
    if np.any((c[..., 1:] == c[..., :-1]) & (c[..., 1:] >= 0)): bad.append("no goal twice in a row of co")
    return bad
def reference(x0, gv, co, aw, ex):
    X = np.full((N, 8, 16, W), -1, np.int64); X[..., :V] = np.asarray(x0).astype(np.float32).astype(np.int64).reshape(N, 8, 16, V)
    GV = gv.astype(np.int64).reshape(N, 8, 16, G); CO = co.astype(np.int64).reshape(N, 8, 16, W); awake = aw.astype(np.int64)
    EX = np.stack([gentries(a) for a in ex]).astype(np.int64); F = np.tile(np.arange(W), (N, 8, 1))
    for step in range(S):
        woken = np.zeros((N, 8, G), bool); sent = np.zeros((N, 8, 16, (N - 1) * E), np.int64)
        for r in range(N):
            for g in range(8):
                x, f, c = X[r, g], F[r, g], CO[r, g]
                k = np.flatnonzero(awake[r, g])[:K]; awake[r, g, k] = 0
                n = f[GV[r, g][:, k]]; o = n[15]; free = x[0, n[:15]] < 0
                cnt = np.add.reduce(free.astype(np.int64), axis=0); M = np.maximum(np.max(x[:, n[:15]], axis=1), 0)
                u = np.add.reduce(np.where(free, n[:15], 0), axis=0)
                todo = x[0, o] < 0
                binds = todo & ((cnt == 0) | np.all(M == 15, axis=0))
                wants = todo & ~binds & (cnt == 1) & np.all(M == 0, axis=0) & (u != o)
                cand = np.flatnonzero(wants)[:A]; a, b = o[cand], u[cand]
                first = np.zeros(len(cand), bool); first[np.unique(b, return_index=True)[1]] = True
                clash = np.any((c[:, a] >= 0) & (c[:, b] >= 0), axis=0)
                ok = first & ~np.isin(b, o[binds | wants]) & ~clash; a, b = a[ok], b[ok]
                x[:, o[binds]] = M[:, binds]
                hit = c[:, o[binds]].reshape(-1); woken[r, g, hit[hit >= 0]] = True
                c[:, b] = np.where(c[:, a] >= 0, c[:, a], c[:, b])
                f[a] = b; F[r, g] = f[f]
                sent[r, g] = x[:, F[r, g][EX[r, g]]]
        for r in range(N):
            for g in range(8):
                come = np.concatenate([sent[r ^ d, far(d, g)][:, (d - 1) * E:d * E] for d in range(1, N)], axis=1)
                new = V + np.flatnonzero((X[r, g, 0, V:] < 0) & (come[0] >= 0)); X[r, g, :, V:] = come
                hit = CO[r, g][:, new].reshape(-1); woken[r, g, hit[hit >= 0]] = True
        awake[woken] = 1
    return {"yx": X.reshape(N, 128, W).astype(np.float32).astype(BF), "yf": F.astype(np.float32), "yw": awake.astype(np.float32), "yc": np.add.reduce(CO, axis=2).astype(np.float32)}

@@ -1,0 +1,664 @@
+from concourse.bass import DstId, RemoteDMATransfer
+from concourse.mybir import AluOpType as ALU, ActivationFunctionType as AF
+
+NV, NE, NG, STEPS = 2880, 64, 1536, 5
+OFF = 256
+IMP = OFF + NV
+DEF = OFF + 3072
+DMP = DEF + 2
+YW = 3392
+CB = 4161.0
+KM = 8192.0
+BIG = 16384.0
+EMPTY = 32767
+STAMP = [2.0 * 8 ** t for t in range(STEPS)]
+DQ = [2, 6, 6, 6, 6]
+DC = [16, 48, 48, 48, 48]
+KA = [7, 7, 7, 8, 10]
+EVEN_FIRST = True
+B2, BT, BL, BA = 9.0, 4.0, 8.0, 3.0
+CY, PE_CY, SEM, ARRIVE, LOOK, GATH, SCAT = 1.04e-3, 0.8e-3, 0.08, 3.0, 0.12, 1.56, 3.8
+
+F, B, I, U = "float32", "bfloat16", "int32", "uint16"
+_SB = {
+    "X0": (NV, B), "GV": (NG, I), "C": (YW, I), "AWI": (96, I), "EXI": (12, I),
+    "Y": (YW, B), "CODE": (YW, B), "MK": (YW, F), "FT": (YW, F), "CF": (YW, F), "YO": (3072, B),
+    "GVP": (NG, F), "ND": (4640, F), "NA": (4640, F), "NM": (256, F), "N16": (256, U),
+    "G": (4096, B), "SC": (4096, B), "MP": (256, B),
+    "WE": (1792, B), "WO": (1792, F), "WO2": (1792, F), "WOB": (1536, B),
+    "AW": (96, B), "PL": (96, B), "PA": (96, F), "PB": (96, F), "PC": (96, F), "OF16": (96, U), "A1": (96, B),
+    "REST": (96, B), "YWF": (96, F), "YCF": (192, F), "YCI": (192, I),
+    "Q": (256, F), "S": (16 * 20, F), "WN": (16, B), "WP": (16, B),
+    "OB16": (16, U), "BW16": (16, U), "UL16": (16, U), "KO16": (16, U),
+    "H": (256, F), "TT": (256, F), "TB16": (256, U),
+    "IP": (192, B), "IH": (192, F), "IT": (192, F), "TI16": (192, U), "IS": (192, B),
+    "GO_": (256, B), "GK": (256, B), "K": (800, B), "KD": (32, B),
+    "LW": (64, F), "L16": (4, U), "EQ": (64, F), "EQS": (64, F), "CC": (64, F), "MN": (32, F), "MT": (32, F),
+    "CFL": (32, F), "FL": (32, B), "XS": (32, F), "BAD": (2, F), "X4": (4, F), "X5": (4, F), "AL16": (4 * STEPS, U),
+    "CN": (32, F), "RV": (32, B), "RF": (32, F), "NEG": (32, B),
+    "EX16": (12, U), "E1": (192, B), "E2": (192, B), "SND": (192 * STEPS, B), "LAND": (192 * STEPS, B),
+    "PI": (8, I), "PC_": (24, F), "IX": (144, F), "IG": (128, F), "IR": (128, F),
+    "IDN": (128, B), "ID8": (128, B), "GON": (128, B), "TRI": (128, B), "PKU": (128, B), "PKO": (128, B),
+    "P1": (128, B), "P2": (128, B), "BCO": (144, B), "BAL": (144, B), "BE": (144, B), "BO": (144, B), "BF": (144, F),
+    "BEF": (144, F), "LC": (128, B), "LY": (128, B), "LT": (128, F), "ZR": (128, B), "R": (4096, B),
+    "D0M": (512, B), "D0S": (256, B), "SEG": (64, F), "S32": (64, F), "PEN": (128, B), "PT": (128, F),
+    "CST": (16, B), "J16": (16, F), "JK": (16, F), "JT": (256, F), "DJ": (4, F), "JB": (8, F),
+    "LM16": (16, U), "LR16": (16, U),
+    "STD": (128 * STEPS, B), "STA": (256 * STEPS, F),
+}
+SCRATCH = {k: ("sbuf", [128, n], d) for k, (n, d) in _SB.items()}
+for _k in range(8):
+    SCRATCH["ps%d" % _k] = ("psum", [128, 512], F)
+NDMA = 24
+SEMAPHORES = ["qv", "qa", "qt", "qg", "sent"] + ["dm%d" % k for k in range(NDMA)] + ["arr%d" % t for t in range(STEPS)]
+
+
+def V(name, a=0, b=None, s=1, p0=0, p1=128, ps=1):
+    if b is None:
+        b = SCRATCH[name][1][1]
+    return ("v", name, a, b, s, p0, p1, ps)
+
+
+def X(win, off):
+    return ("x", win, off)
+
+
+def rank_program(g, core, T, topo):
+    rank = T.rank_of(core)
+    if rank is None:
+        return
+    cores = list(T.cores)
+    N = len(cores)
+    eng = {"v": g.vector, "a": g.scalar, "t": g.tensor, "g": g, "s": g.sync}
+    ops = []
+    hist = {}
+    ndma, pool, prev, sends, bump = [0], [], {}, [], [0.0, 0.0]
+
+    def ap(x):
+        if not isinstance(x, tuple):
+            return x
+        if x[0] == "x":
+            return ap(x[1]).indirect(ap(x[2]))
+        return T[x[1]][x[5]:x[6]:x[7], x[2]:x[3]:x[4]] if (x[4] != 1 or x[7] != 1) else T[x[1]][x[5]:x[6], x[2]:x[3]]
+
+    def width(x):
+        return 16 * (x[2][3] - x[2][2]) if x[0] == "x" else len(range(x[2], x[3], x[4]))
+
+    def cost(q, outs, ins, kind, per):
+        if kind != "c":
+            return 0.1 if kind == "d" else 0.5
+        aps = [x for x in outs + ins if isinstance(x, tuple)]
+        n = width(outs[0])
+        if q == "t":
+            return max(64, n) * (4 if SCRATCH[ins[0][1]][2] == F else 1) * PE_CY
+        if q == "g":
+            return 0.16 + 2 * n * CY
+        if outs[0][0] == "x":
+            return 0.07 + SCAT * n * CY
+        if ins and ins[0][0] == "x":
+            return 0.07 + GATH * n * CY
+        if per == 2 and any(x[1].startswith("ps") for x in aps[1:]):
+            per = 1
+        if per == 1 and q == "v" and all(SCRATCH[x[1]][2] in (B, U) for x in aps if width(x) > 1):
+            per = 0.5
+        return max(64, n * per) * CY
+
+    def add(q, emit, outs, ins, kind="c", ext=None, per=1, lat=0.0):
+        acc = []
+        for lst, w in ((outs, True), (ins, False)):
+            for x in lst:
+                if not isinstance(x, tuple):
+                    continue
+                if x[0] == "x":
+                    acc.append((x[1], w, False))
+                    acc.append((x[2], False, False))
+                else:
+                    acc.append((x, w, w))
+        i = len(ops)
+        deps, order = set(), set()
+        for x, w, _ in acc:
+            name, lo, hi = x[1], x[2], x[3]
+            bank = name.startswith("ps")
+            for (l2, h2, j, w2, pa, pb, s2) in hist.get(name, []):
+                same = ops[j][0] == q and ops[j][3] == "c" and kind == "c"
+                if bank and same and q == "t":
+                    order.add(j)
+                elif bank and not same:
+                    deps.add(j)
+                elif l2 < hi and lo < h2 and (w or w2) and pa < x[6] and x[5] < pb:
+                    if s2 > 1 and s2 == x[4] and (lo - l2) % s2:
+                        continue
+                    if not same or q != "t":
+                        deps.add(j)
+        for x, w, whole in acc:
+            h = hist.setdefault(x[1], [])
+            if w and x[4] == 1 and x[5] == 0 and x[6] == 128 and x[7] == 1:
+                h[:] = [e for e in h if not (x[2] <= e[0] and e[1] <= x[3] and (e[2] in deps or e[2] in order))]
+            h.append((x[2], x[3], i, w, x[5], x[6], x[4]))
+        if q == "g" and kind == "c":
+            if pool:
+                deps.add(pool[-1])
+            pool.append(i)
+        if q == "g" or (kind == "d" and lat != 2.5):
+            if q in prev:
+                order.add(prev[q])
+            prev[q] = i
+        if ext is not None:
+            order.add(sends[-1])
+        if kind == "r":
+            sends.append(i)
+            lat = ARRIVE
+        ops.append([q, emit, deps, kind, False, ext, order, cost(q, outs, ins, kind, per), lat, bump[0], bump[1]])
+        return i
+
+    def cp(out, in_):
+        add("v", lambda e: e.tensor_copy(ap(out), ap(in_)), [out], [in_])
+
+    def tt(out, a, b, op):
+        add("v", lambda e: e.tensor_tensor(ap(out), ap(a), ap(b), op), [out], [a, b], per=2)
+
+    def ts(out, a, s1, op0, s2=None, op1=None, after=()):
+        if op1 is None:
+            add("v", lambda e: e.tensor_scalar(ap(out), ap(a), ap(s1), None, op0), [out], [a, s1] + list(after))
+        else:
+            add("v", lambda e: e.tensor_scalar(ap(out), ap(a), ap(s1), ap(s2), op0, op1), [out], [a, s1, s2] + list(after))
+
+    def scan(out, d0, d1, init, op0, op1):
+        add("v", lambda e: e.tensor_tensor_scan(ap(out), ap(d0), ap(d1), init, op0, op1), [out], [d0, d1])
+
+    def trn(out, in_):
+        add("v", lambda e: e.transpose(ap(out), ap(in_)), [out], [in_])
+
+    def mset(out, c):
+        add("v", lambda e: e.memset(ap(out), c), [out], [])
+
+    def act(out, in_, func, bias=None, scale=None):
+        if bias is None:
+            add("a", lambda e: e.activation(ap(out), ap(in_), func), [out], [in_])
+        else:
+            add("a", lambda e: e.activation(ap(out), ap(in_), func, bias=ap(bias), scale=ap(scale)), [out], [in_, bias, scale])
+
+    def mm(out, lhsT, rhs, start, stop):
+        add("t", lambda e: e.matmul(ap(out), ap(lhsT), ap(rhs), start, stop), [out], [lhsT, rhs])
+
+    def iota(out, pat, base, ch):
+        if SCRATCH[out[1]][2] == I:
+            add("g", lambda e: e.iota(ap(out), pat, base, ch), [out], [])
+        else:
+            add("g", lambda e: e.iota(ap(out), pat, base, ch, allow_small_or_imprecise_dtypes=True), [out], [])
+
+    def dma(q, out, in_, lat=2.2):
+        add(q, lambda e: e.dma_start(ap(out), ap(in_)), [out], [in_], kind="d", lat=lat)
+
+    def col(k):
+        return V("PC_", k, k + 1)
+
+    def S_(k):
+        return V("S", 16 * k, 16 * k + 16)
+
+    CIMP, JG = V("ps5", 0, 192), V("ps5", 192, 288)
+
+    dma("s", V("AWI"), T.aw[:])
+    dma("s", V("GV"), T.gv[:], 6.5)
+    dma("a", V("X0"), T.x0[:], 8.0)
+    dma("a", V("EXI"), T.ex[:])
+    dma("a", V("C", OFF, DEF), T.co[:], 12.0)
+
+    iota(V("PI", 0, 1), [[0, 1]], 0, 1)
+    iota(V("IX"), [[1, 144]], 0, 0)
+    mset(V("ZR", p0=0, p1=32), 1.0)
+    iota(V("ZR", p0=32, p1=64), [[-64, 2], [0, 64]], -64, -128)
+    iota(V("ZR", p0=64, p1=96), [[0, 2], [-1, 64]], -1, 0)
+    iota(V("IR"), [[0, 8], [1, 16]], 0, 0)
+    iota(V("IG"), [[1, 8], [0, 16]], 0, 0)
+    dma("s", V("R", p0=0, p1=3), V("ZR", p0=0, p1=96))
+    dma("s", V("R", 0, 4096, 1, 3, 5), V("ZR", p0=32, p1=96))
+    iota(V("ND", 0, 256), [[0, 256]], 0, 0)
+    iota(V("NA", 0, 256), [[0, 256]], 0, 0)
+    iota(V("JT"), [[1, 256]], NG, 0)
+    iota(V("STA", 0, 256), [[0, 256]], int(STAMP[0]), 0)
+    iota(V("STD", 0, 128), [[0, 128]], int(STAMP[0]), 0)
+    iota(V("MK"), [[0, YW]], 0, 0)
+    iota(V("MK", DEF, DEF + 1), [[0, 1]], 1000000, 0)
+    iota(V("WO"), [[0, 1792]], 0, 0)
+    iota(V("WE"), [[0, 1792]], 0, 0)
+    iota(V("WO2"), [[0, 1792]], 0, 0)
+    mset(V("D0M"), 1.0)
+    mset(V("D0S"), 1.0)
+    mset(V("CST"), -240.0 * KM)
+    mset(V("Y", 0, OFF), 0.0)
+    mset(V("C", 0, OFF), EMPTY)
+    mset(V("C", DEF, YW), EMPTY)
+    mset(V("S32"), 1.0)
+    mset(V("NEG"), -1.0)
+    mset(V("D0M", 0, 512, 16), 0.0)
+    mset(V("D0S", 0, 256, 16), 0.0)
+    mset(V("D0S", 15, 256, 16), 0.0)
+    mset(V("S32", 32, 33), 0.0)
+    ts(V("PI", 1, 2), V("PI", 0, 1), 15, ALU.bitwise_and)
+    ts(V("PI", 2, 3), V("PI", 0, 1), 4, ALU.arith_shift_right)
+    ts(V("PI", 3, 4), V("PI", 0, 1), 5, ALU.arith_shift_right)
+    ts(V("PI", 4, 5), V("PI", 0, 1), 7, ALU.bitwise_and)
+    cp(V("PC_", 0, 5), V("PI", 0, 5))
+    ts(col(5), col(1), 96.0, ALU.mult, 1536.0, ALU.add)
+    ts(col(6), col(2), 16.0, ALU.mult, 15.0, ALU.add)
+    ts(col(7), col(1), 2.5, ALU.is_lt)
+    ts(col(8), col(1), 16.0, ALU.mult, CB, ALU.add)
+    ts(col(9), col(1), 256.0, ALU.mult, 14.25, ALU.add)
+    ts(col(10), col(1), 7.5, ALU.is_gt, 0.25, ALU.add)
+    ts(col(17), col(2), -16.0, ALU.mult, 112.0, ALU.add)
+    ts(col(19), col(1), 0.5, ALU.is_lt)
+    ts(col(20), col(3), 32.0, ALU.mult, 15.0, ALU.add)
+    ts(col(21), col(3), 32.0, ALU.mult, 31.0, ALU.add)
+    ts(col(11), col(4), 32.0, ALU.mult, col(10), ALU.add)
+    ts(col(12), col(1), 0.5, ALU.is_gt, col(7), ALU.mult)
+    ts(col(13), col(1), 4.5, ALU.is_lt, col(7), ALU.subtract)
+    tt(col(17), col(17), col(1), ALU.add)
+    ts(V("ID8"), V("IX", 0, 128), col(0), ALU.is_equal, KM, ALU.mult)
+    ts(col(14), col(12), -1.0, ALU.mult)
+    ts(col(15), col(13), -1.0, ALU.mult)
+    ts(col(16), col(12), -BIG, ALU.mult)
+    ts(col(18), col(17), 111.5, ALU.is_gt, -128.0, ALU.mult)
+    ts(V("LT"), V("IX", 0, 128), col(0), ALU.is_gt)
+    ts(col(18), col(18), col(17), ALU.add, 16.0, ALU.add)
+    ts(V("LC", p1=32), V("IR", p1=32), V("PC_", 0, 1, p1=32), ALU.is_equal)
+    ts(V("H", 0, 128, p1=1), V("IR", p1=1), 4.5, ALU.is_gt, -64.0, ALU.mult)
+    ts(V("PT", p1=1), V("IR", p1=1), 0.5, ALU.is_lt, -4096.0, ALU.mult)
+    ts(JG, V("IX", 0, 96), col(5), ALU.add)
+    tt(V("LC", p1=1), V("H", 0, 128, p1=1), V("PT", p1=1), ALU.add)
+    ts(V("GON"), V("IG"), col(2), ALU.is_equal)
+    cp(V("LY", p1=32), V("LC", p1=32))
+    tt(V("TRI"), V("LT"), V("GON"), ALU.mult)
+    ts(V("LY", p1=1), V("LC", p1=1), KM, ALU.add)
+    for k in range(7):
+        a, b = 512 * k, min(512 * k + 512, YW)
+        pk = ("ps0", "ps1", "ps2")[k % 3]
+        mm(V(pk, 0, b - a), V("LC", p1=5), V("R", a, b, p1=5), True, True)
+        act(V("CODE", a, b), V(pk, 0, b - a), AF.Copy)
+    act(V("Y", IMP, YW), V("CODE", IMP, YW), AF.Copy)
+
+    def ranks(t):
+        if t == 0:
+            cp(V("AW"), V("AWI"))
+        else:
+            ts(V("AW"), V("ps2", 0, 96), 0.75 * STAMP[t - 1], ALU.is_ge)
+        scan(V("PL"), V("AW"), V("AW"), 0.0, ALU.add, ALU.max)
+        mm(V("ps3", 0, 1), V("TRI"), V("PL", 95, 96), True, True)
+        ts(V("PA"), V("AW"), -BIG, ALU.mult, BIG, ALU.add)
+        tt(V("PB"), V("PA"), V("PL"), ALU.add)
+        tt(V("PC"), V("PB"), JG, ALU.min)
+        ts(V("OF16"), V("PC"), V("ps3", 0, 1), ALU.add, -0.75, ALU.add)
+
+    def compaction(t):
+        act(X(V("NA"), V("OF16", DC[t], 96)), V("GVP", 16 * DC[t], NG), AF.Silu)
+        cp(X(V("ND"), V("OF16", 0, DC[t])), V("GVP", 0, 16 * DC[t]))
+
+    ranks(0)
+    ts(V("IDN"), V("IX", 0, 128), col(0), ALU.is_equal)
+    ts(V("BCO"), V("IX"), col(6), ALU.is_equal, col(7), ALU.mult)
+    ts(V("BAL"), V("IX"), col(6), ALU.is_equal, KM, ALU.mult)
+    ts(V("J16"), V("IX", 0, 16), col(8), ALU.add)
+    ts(V("LM16"), V("IX", 0, 16), 16.0, ALU.mult, col(9), ALU.add)
+    ts(V("LR16"), V("IX", 0, 16), 2.0, ALU.mult, col(11), ALU.add)
+    ts(V("JK"), V("J16"), 300.0 - CB, ALU.add)
+    for q in range(16):
+        ts(V("GVP", q, NG, 16), V("GV", 96 * q, 96 * q + 96), float(OFF), ALU.add)
+    compaction(0)
+    for k in range(6):
+        a, b = 480 * k, 480 * k + 480
+        pk = ("ps4", "ps6", "ps7")[k % 3]
+        mm(V(pk, 0, 480), V("LY", p1=5), V("R", OFF + a, OFF + b, p1=5), True, False)
+        mm(V(pk, 0, 480), V("ID8"), V("X0", a, b), False, True)
+        tt(V("Y", OFF + a, OFF + b), V("X0", a, b), V(pk, 0, 480), ALU.min)
+
+    def grant_constants():
+        ts(V("PKU"), V("GON"), col(14), ALU.mult)
+        ts(V("PKO"), V("GON"), col(13), ALU.mult)
+        ts(V("PEN", 0, 64), V("IR", 0, 64), col(1), ALU.not_equal, -BIG, ALU.mult)
+        ts(V("PEN", 64, 96), V("IX", 0, 32), col(1), ALU.is_ge, BIG, ALU.mult)
+        ts(V("PT", 32, 64), V("IX", 0, 32), -16.0, ALU.add, col(1), ALU.is_ge)
+        ts(V("SEG"), V("IR", 0, 64), 0.5, ALU.is_lt, -4.0 * BIG, ALU.mult)
+        ts(V("PEN", 96, 128), V("PT", 32, 64), BIG, ALU.mult)
+        ts(V("JB"), V("IX", 0, 8), 16.0, ALU.mult, col(1), ALU.add)
+        ts(V("KD", 0, 1), V("CODE", DEF, DEF + 1), col(15), ALU.mult, col(16), ALU.add)
+        ts(V("DJ", 0, 2), V("JB", 0, 2), float(DMP), ALU.add)
+        ts(V("DJ", 2, 4), V("JB", 0, 2), float(DMP), ALU.add)
+        tt(col(22), V("KD", 0, 1), V("CODE", DEF, DEF + 1), ALU.max)
+        ts(V("JB"), V("JB"), float(NG), ALU.add)
+        ts(V("EX16"), V("EXI"), OFF + 0.25, ALU.add)
+        ts(V("KD"), V("IX", 0, 32), 0.0, ALU.mult, col(22), ALU.add)
+        ts(V("P1"), V("IX", 0, 128), col(17), ALU.is_equal)
+        ts(V("P2"), V("IX", 0, 128), col(18), ALU.is_equal)
+
+    def wake_constants():
+        cp(CIMP, V("CODE", IMP, DEF))
+        ts(V("BE"), V("IX"), col(20), ALU.is_equal, col(19), ALU.mult)
+        ts(V("BEF"), V("IX"), col(20), ALU.is_equal, col(19), ALU.mult)
+        ts(V("BO"), V("IX"), col(21), ALU.is_equal, col(19), ALU.mult)
+        ts(V("BF"), V("IX"), col(6), ALU.is_equal)
+
+    masks, used = {}, set()
+    for p in sorted([cores[rank ^ d] for d in range(1, N)], key=lambda c: len(topo.engines(core, c))):
+        assert topo.may_write(core, p)
+        es = [e for e in topo.engines(core, p) if e not in used][:4]
+        used.update(es)
+        masks[p] = sum(1 << e for e in es)
+    n_arr = 4 * (N - 1)
+
+    def send(t):
+        def emit(e):
+            trs = []
+            for d in range(1, N):
+                p = cores[rank ^ d]
+                rid, pid, _ = topo.addr(p)
+                a = 192 * t + NE * (d - 1)
+                trs.append(RemoteDMATransfer(dst_ids=[DstId(rid=rid, pnc=pid)], dma_engine_mask=masks[p],
+                                             remote_sem=T.sem["arr%d" % t], src=T["SND"][:, a:a + NE],
+                                             dst=T["LAND"][:, a:a + NE]))
+            e.remote_dma_fused(trs, local_sem=T.sem.sent)
+            return None
+        add("g", emit, [], [V("SND", 192 * t, 192 * t + 192)], kind="r")
+
+    def refresh(tab, tmp, t, fill):
+        for k in range(t, -1, -1):
+            cp(V(tmp), X(V(tab), V("AL16", 4 * k, 4 * k + 2)))
+            fill()
+            cp(X(V(tab), V("AL16", 4 * k + 2, 4 * k + 4)), V(tmp))
+            fill()
+
+    for t in range(STEPS):
+        std, sta = V("STD", 128 * t, 128 * t + 128), V("STA", 256 * t, 256 * t + 256)
+        ct = "C" if t == 0 else "CF"
+        rows = list(range(KA[t], 16))
+
+        def wake_row(rows=rows, std=std):
+            if rows:
+                r = rows.pop(0)
+                cp(X(V("WE"), V("TB16", 8 * r, 8 * r + 8)), std)
+
+        dq = DQ[t]
+        for a, b in ((16 * dq, 16 * dq + 64), (0, 16 * dq), (16 * dq + 64, 256)):
+            tt(V("NM", a, b), V("ND", a, b), V("NA", a, b), ALU.max)
+            bump[1] = 3.0
+            ts(V("N16", a, b), V("NM", a, b), 0.25, ALU.add)
+            bump[1] = 0.0
+        if t + 1 < STEPS:
+            iota(V("ND", 0, 256), [[0, 256]], 0, 0)
+            iota(V("NA", 0, 256), [[0, 256]], 0, 0)
+        for q in range(0, 16, 2):
+            src = X(V("Y"), V("N16", 16 * q, 16 * q + 32))
+            if q < dq:
+                cp(V("G", 256 * q, 256 * q + 512), src)
+            else:
+                act(V("G", 256 * q, 256 * q + 512), src, AF.Copy)
+        mm(V("ps1", 0, 16), V("IDN"), V("CST"), True, False)
+        for q in range(0, 16, 2):
+            scan(V("SC", 256 * q, 256 * q + 512), V("D0M"), V("G", 256 * q, 256 * q + 512), 0.0, ALU.mult, ALU.max)
+        order = sorted(range(16), key=lambda q: (q // 2 + 0.5 if q < dq else (q - dq) // 2, q))
+        for n, q in enumerate(order):
+            mm(V("ps0", 0, 256), V("BCO", 15 - q, 143 - q), V("G", 256 * q, 256 * q + 256), n == 0, n == 15)
+        for q in range(16):
+            mm(V("ps1", 0, 16), V("BAL", 15 - q, 143 - q), V("SC", 256 * q + 14, 256 * q + 256, 16), False, q == 15)
+        act(V("MP"), X(V("SC"), V("LM16")), AF.Copy)
+        ts(V("A1"), V("PL"), V("ps3", 0, 1), ALU.add, 256.5, ALU.is_gt)
+        bump[0] = BA
+        if t == 0:
+            for k in range(4):
+                ts(V("C", OFF + 768 * k, OFF + 768 * k + 768), V("C", OFF + 768 * k, OFF + 768 * k + 768), EMPTY,
+                   ALU.bitwise_and)
+        bump[0] = 0.0
+        bump[1] = 6.0
+        tt(V("REST"), V("A1"), V("AW"), ALU.mult)
+        bump[1] = 0.0
+        scan(V("Q"), V("D0S"), V("ps0", 0, 256), 0.0, ALU.mult, ALU.add)
+        Sn, So = V("Q", 14, 256, 16), V("Q", 15, 256, 16)
+        ts(S_(0), Sn, 0.0, ALU.min)
+        tt(S_(5), Sn, So, ALU.not_equal)
+        tt(S_(6), Sn, So, ALU.max)
+        tt(S_(1), S_(0), V("ps1", 0, 16), ALU.max)
+        ts(S_(4), V("ps1", 0, 16), 240.0 * KM - 8000.0, ALU.add)
+        tt(S_(2), S_(1), So, ALU.subtract)
+        tt(S_(8), S_(5), S_(6), ALU.mult)
+        tt(S_(3), S_(2), V("J16"), ALU.max)
+        tt(S_(7), Sn, S_(4), ALU.is_gt)
+        ts(V("OB16"), S_(3), 0.25 - CB, ALU.add)
+        tt(S_(9), S_(7), S_(8), ALU.mult)
+        tt(V("H"), X(V(ct), V("OB16")), V("JT"), ALU.min)
+        ts(V("WN"), S_(9), -1000.0, ALU.is_lt, -1.0, ALU.mult)
+        trn(V("TT"), V("H"))
+        tt(S_(10), V("WN"), So, ALU.mult)
+        scan(V("WP"), V("CST"), V("WN"), 0.0, ALU.max, ALU.subtract)
+        tt(S_(11), S_(10), S_(3), ALU.max)
+        mm(V("ps3", 0, 1), V("TRI"), V("WP", 15, 16), True, True)
+        tt(S_(12), V("WN"), Sn, ALU.mult)
+        ts(V("BW16"), S_(11), 0.25 - CB, ALU.add)
+        bump[1] = BT
+        ts(V("TB16"), X(V("TT"), V("LR16")), 0.25, ALU.add)
+        bump[1] = 0.0
+        act(V("GO_"), X(V("CODE"), V("BW16")), AF.Identity, bias=col(16), scale=col(15))
+        act(X(V("MK"), V("BW16")), sta, AF.Silu)
+        for r in range(16, 32):
+            bump[0] = -0.6 * min(r - 16, KA[t])
+            act(X(V("WO"), V("TB16", 8 * r, 8 * r + 8)), V("STA", 256 * t, 256 * t + 128), AF.Silu)
+        for r in range(KA[t]):
+            bump[0] = B2 - 0.6 * r
+            act(X(V("WO2"), V("TB16", 8 * r, 8 * r + 8)), V("STA", 256 * t, 256 * t + 128), AF.Silu)
+        bump[0] = 0.0
+        if t == 0:
+            grant_constants()
+        ts(V("UL16"), S_(12), 0.25 - CB, ALU.add)
+        ts(S_(13), V("WN"), BIG, ALU.mult, BIG, ALU.add)
+        cp(V("K", 0, 32), V("KD"))
+        tt(S_(14), S_(13), V("WP"), ALU.add)
+        tt(V("GK"), X(V("CODE"), V("UL16")), V("GO_"), ALU.max)
+        tt(S_(15), S_(14), V("JK"), ALU.min)
+        ts(V("KO16"), S_(15), V("ps3", 0, 1), ALU.add, -0.75, ALU.add)
+        cp(X(V("K"), V("KO16")), V("GK"))
+        mm(V("ps4", 0, 128), V("IDN"), V("PEN"), True, False)
+        mm(V("ps4", 0, 32), V("PKU"), V("K", 0, 32), False, False)
+        mm(V("ps4", 32, 64), V("PKO"), V("K", 0, 32), False, False)
+        mm(V("ps4", 64, 96), V("PKU"), V("K", 0, 32), False, False)
+        mm(V("ps4", 96, 128), V("PKU"), V("K", 0, 32), False, True)
+        cp(X(V("Y"), V("OB16")), V("MP"))
+        scan(V("LW"), V("SEG"), V("ps4", 0, 64), 0.0, ALU.add, ALU.max)
+        ts(V("L16"), V("LW", 15, 64, 16), 0.25 - 65.0, ALU.add)
+        ts(V("EQ", 0, 32), V("ps4", 64, 96), V("LW", 15, 16), ALU.is_equal)
+        ts(V("EQ", 32, 64), V("ps4", 96, 128), V("LW", 31, 32), ALU.is_equal)
+        cp(V("CC"), X(V(ct), V("L16")))
+        ts(V("MT"), X(V("MK"), V("L16", 0, 2)), -0.75 * STAMP[t], ALU.add, -10000.0, ALU.mult)
+        tt(V("MN"), V("CC", 0, 32), V("CC", 32, 64), ALU.max)
+        scan(V("EQS"), V("S32"), V("EQ"), 0.0, ALU.mult, ALU.max)
+        tt(V("CFL"), V("MN"), V("MT"), ALU.min)
+        tt(V("CN"), V("CC", 0, 32), V("CC", 32, 64), ALU.min)
+        ts(V("FL"), V("CFL"), 2048.0, ALU.is_lt)
+        mm(V("ps3", 0, 32), V("IDN"), V("PEN", 0, 32), True, False)
+        mm(V("ps3", 0, 32), V("GON"), V("FL"), False, True)
+        wake_row()
+        scan(V("XS"), V("SEG", 0, 32), V("ps3", 0, 32), 0.0, ALU.add, ALU.max)
+        tt(V("BAD"), V("XS", 15, 32, 16), V("EQS", 31, 64, 32), ALU.max)
+        ts(V("BAD"), V("BAD"), BIG, ALU.mult, -65.0, ALU.add)
+        tt(V("X4", 0, 2), V("LW", 15, 32, 16), V("BAD"), ALU.add)
+        tt(V("X4", 2, 4), V("LW", 47, 64, 16), V("BAD"), ALU.add)
+        tt(V("X5"), V("X4"), V("DJ"), ALU.min)
+        ts(V("AL16", 4 * t, 4 * t + 4), V("X5"), 0.25, ALU.add)
+        refresh("Y", "RV", t, lambda: None)
+        cp(V("E1"), X(V("Y"), V("EX16")))
+        bump[0] = 4.0 if t + 1 == STEPS else 0.0
+        cp(X(V(ct), V("AL16", 4 * t, 4 * t + 2)), V("CN"))
+        bump[0] = 0.0
+        ts(V("E2"), V("E1"), KM, ALU.mult, 0.0, ALU.min)
+        for d in range(1, N):
+            pm = V(("IDN", "P1", "P2")[d % 3])
+            a = NE * (d - 1)
+            mm(V("ps6", a, a + NE), pm, V("E1", a, a + NE), True, False)
+            mm(V("ps6", a, a + NE), pm, V("E2", a, a + NE), False, True)
+        wake_row()
+        cp(V("SND", 192 * t, 192 * t + 192), V("ps6", 0, 192))
+        send(t)
+        if t == 0:
+            for k in range(1, STEPS):
+                iota(V("STA", 256 * k, 256 * k + 256), [[0, 256]], int(STAMP[k]), 0)
+                iota(V("STD", 128 * k, 128 * k + 128), [[0, 128]], int(STAMP[k]), 0)
+            wake_constants()
+        if t == 1:
+            iota(V("FT"), [[1, YW]], -OFF, 0)
+        if t + 1 == STEPS:
+            bump[0] = BL
+            for k in range(STEPS):
+                cp(X(V("Y"), V("AL16", 4 * k + 2, 4 * k + 4)), V("NEG"))
+            for a, b in ((0, 1440), (1440, NV)):
+                ts(V("YO", a, b), V("Y", OFF + a, OFF + b), -1.0, ALU.max)
+                dma("s", T.yx[:, a:b], V("YO", a, b), 2.5)
+            refresh("FT", "RF", t, lambda: None)
+            dma("s", T.yf[:], V("FT", OFF, DEF, p0=0, p1=128, ps=16), 2.5)
+            bump[0] = 0.0
+            for q in range(16):
+                mm(V("ps7", 0, 192), V("BF", 15 - q, 143 - q), V("CF", OFF + 192 * q, OFF + 192 * q + 192), q == 0, q == 15)
+        while len(rows) > 3:
+            wake_row()
+        land = V("LAND", 192 * t, 192 * t + 192)
+        add("v", lambda e, land=land: e.tensor_scalar(ap(V("IS")), ap(land), -1.0, 0.0, ALU.mult, ALU.max), [V("IS")], [],
+            ext=("arr%d" % t, n_arr))
+        mm(V("ps6", 0, 192), V("IDN"), V("IS"), True, t == 0)
+        if t > 0:
+            mm(V("ps6", 0, 192), V("IDN"), V("IP"), False, True)
+        if t + 1 < STEPS:
+            add("v", lambda e, land=land: e.tensor_tensor(ap(V("Y", IMP, DEF)), ap(land), ap(CIMP), ALU.max),
+                [V("Y", IMP, DEF)], [land, CIMP, V("IS")])
+        wake_row()
+        tt(V("IH"), V(ct, IMP, DEF), V("ps6", 0, 192), ALU.add)
+        wake_row()
+        trn(V("IT"), V("IH"))
+        wake_row()
+        for b in range(6):
+            ts(V("TI16", b, 192, 6), V("IT", 32 * b, 32 * b + 32), V("JB", b, b + 1), ALU.min, 0.25, ALU.add)
+        for r in range(16, 32):
+            act(X(V("WO"), V("TI16", 6 * r, 6 * r + 6)), V("STA", 256 * t, 256 * t + 96), AF.Silu)
+        for k in range(3):
+            act(V("WOB", 512 * k, 512 * k + 512), V("WO", 512 * k, 512 * k + 512), AF.Copy)
+        irows = list(range(16))
+
+        def import_row(irows=irows, t=t):
+            if irows:
+                r = irows.pop(0)
+                cp(X(V("WE"), V("TI16", 6 * r, 6 * r + 6)), V("STD", 128 * t, 128 * t + 96))
+
+        if t + 1 < STEPS:
+            ts(V("IP"), land, 0.0, ALU.is_ge, BIG, ALU.mult, after=[V("IS")])
+            refresh("Y", "RV", t, import_row)
+        else:
+            ts(V("YO", NV, 3072), land, -1.0, ALU.max, after=[V("IS")])
+            dma("s", T.yx[:, NV:3072], V("YO", NV, 3072), 2.5)
+            ts(V("YCI"), V("ps7", 0, 192), 16.0, ALU.add)
+            ts(V("YCI"), V("YCI"), EMPTY, ALU.bitwise_and)
+            ts(V("YCF"), V("YCI"), -16.0, ALU.add)
+            dma("s", T.yc[:], V("YCF"), 2.5)
+        while irows:
+            import_row()
+        mm(V("ps2", 0, 96), V("ID8"), V("REST"), True, False)
+        if KA[t]:
+            for q in range(16):
+                mm(V("ps2", 0, 96), V("BEF", 15 - q, 143 - q), V("WO2", 96 * q, 96 * q + 96), False, False)
+        two = [("BO", "WOB"), ("BE", "WE")]
+        for n, (sel, win) in enumerate(two[::-1] if EVEN_FIRST else two):
+            for q in range(16):
+                mm(V("ps2", 0, 96), V(sel, 15 - q, 143 - q), V(win, 96 * q, 96 * q + 96), False, n == 1 and q == 15)
+        if t == 0:
+            for k in range(8):
+                cp(V("CF", 424 * k, 424 * k + 424), V("C", 424 * k, 424 * k + 424))
+        if t + 1 < STEPS:
+            ranks(t + 1)
+            compaction(t + 1)
+        else:
+            ts(V("YWF"), V("ps2", 0, 96), 0.75 * STAMP[t], ALU.is_ge)
+            dma("s", T.yw[:], V("YWF"), 2.5)
+
+    n_ops = len(ops)
+    succ = [[] for _ in ops]
+    for i, o in enumerate(ops):
+        for j in o[2] | o[6]:
+            succ[j].append(i)
+
+    def gap(j, i):
+        if j in ops[i][2]:
+            return ops[j][8] + SEM
+        return ops[j][8] if ops[j][3] == "r" and ops[i][5] is not None else 0.0
+
+    prio = [0.0] * n_ops
+    for i in range(n_ops - 1, -1, -1):
+        prio[i] = ops[i][7] + ops[i][10] + max([ops[i][8]] + [gap(i, k) + prio[k] for k in succ[i]])
+    left = [len(o[2] | o[6]) for o in ops]
+    ready = [0.0] * n_ops
+    pend = {q: [] for q in eng}
+    free = {q: 0.0 for q in eng}
+    for i in range(n_ops):
+        if not left[i]:
+            pend[ops[i][0]].append(i)
+    prio = [p + o[9] for p, o in zip(prio, ops)]
+    seq = []
+    while len(seq) < n_ops:
+        now, q = min((max(free[q], min(ready[i] for i in pend[q])), q) for q in eng if pend[q])
+        i = max((i for i in pend[q] if ready[i] <= now + LOOK), key=lambda i: (prio[i], -i))
+        pend[q].remove(i)
+        seq.append(i)
+        free[q] = max(now, ready[i]) + ops[i][7]
+        for k in succ[i]:
+            ready[k] = max(ready[k], free[q] + gap(i, k))
+            left[k] -= 1
+            if not left[k]:
+                pend[ops[k][0]].append(k)
+    place = {j: i for i, j in enumerate(seq)}
+    ops = [ops[j] for j in seq]
+    for o in ops:
+        o[2] = {place[j] for j in o[2]}
+
+    last, tops = {}, []
+    for i, o in enumerate(ops):
+        if o[3] == "c":
+            last[o[0]] = i
+        top = {}
+        for j in o[2]:
+            if ops[j][3] == "c":
+                top[ops[j][0]] = max(top.get(ops[j][0], -1), j)
+        tops.append(top)
+    seen = {}
+    for i, o in enumerate(ops):
+        for q, j in tops[i].items():
+            if seen.get((o[0], q), -1) < j:
+                seen[(o[0], q)] = j
+                ops[j][4] = True
+    for i in last.values():
+        ops[i][4] = True
+    cnt = {"v": 0, "a": 0, "t": 0, "g": 0}
+    val, waited, seen = {}, {}, {}
+    for i, o in enumerate(ops):
+        if o[3] == "c" and o[4]:
+            cnt[o[0]] += 1
+            val[i] = ("q" + o[0], cnt[o[0]])
+        elif o[3] == "d":
+            val[i] = ("dm%d" % ndma[0], 16)
+            ndma[0] += 1
+    for i, o in enumerate(ops):
+        e = eng[o[0]]
+        need = {}
+        for j in o[2]:
+            if ops[j][3] == "d":
+                need[val[j][0]] = 16
+        for q, j in tops[i].items():
+            if seen.get((o[0], q), -1) < j:
+                seen[(o[0], q)] = j
+                need[val[j][0]] = val[j][1]
+        if o[5] is not None:
+            need[o[5][0]] = o[5][1]
+        for s in sorted(need):
+            if waited.get((o[0], s), 0) < need[s]:
+                e.wait_ge(T.sem[s], need[s])
+                waited[(o[0], s)] = need[s]
+        r = o[1](e)
+        if i in val:
+            r.then_inc(T.sem[val[i][0]], 16 if o[3] == "d" else 1)
+    g.wait_ge(T.sem.sent, n_arr * STEPS)
+    for q in cnt:
+        g.sync.wait_ge(T.sem["q" + q], cnt[q])
+    for k in range(ndma[0]):
+        g.sync.wait_ge(T.sem["dm%d" % k], 16)

@@ -12,20 +12,24 @@ KM = 8192.0
 BIG = 16384.0
 EMPTY = 32767
 STAMP = [2.0 * 8 ** t for t in range(STEPS)]
-DQ = [2, 6, 6, 6, 6]
-DC = [16, 48, 48, 48, 48]
-KA = [7, 7, 7, 8, 10]
+DQ = [1, 6, 6, 6, 6]
+DC = [20, 48, 50, 50, 46]
+KA = [5, 5, 5, 5, 7]
 EVEN_FIRST = True
-B2, BT, BL, BA = 9.0, 4.0, 8.0, 3.0
-CY, PE_CY, SEM, ARRIVE, LOOK, GATH, SCAT = 1.04e-3, 0.8e-3, 0.08, 3.0, 0.12, 1.56, 3.8
+W2L = 12
+PAA, NMP = True, True
+BT2, NM2, BFT = 3.0, False, 0.0
+CFK = [0, 3, 6, 8, 8, 8]
+B2, BT, BL, BA = 15.0, 6.0, 8.0, 0.0
+CY, PE_CY, SEM, ARRIVE, LOOK, GATH, SCAT = 1.04e-3, 0.8e-3, 0.06, 4.5, 0.09, 1.56, 3.8
 
 F, B, I, U = "float32", "bfloat16", "int32", "uint16"
 _SB = {
     "X0": (NV, B), "GV": (NG, I), "C": (YW, I), "AWI": (96, I), "EXI": (12, I),
-    "Y": (YW, B), "CODE": (YW, B), "MK": (YW, F), "FT": (YW, F), "CF": (YW, F), "YO": (3072, B),
+    "Y": (YW, B), "CODE": (YW, B), "OWG": (256, B), "MPA": (256, B), "OW16": (16, U), "SCF": (16, F), "FT": (YW, F), "CF": (YW, F), "YO": (3072, B),
     "GVP": (NG, F), "ND": (4640, F), "NA": (4640, F), "NM": (256, F), "N16": (256, U),
     "G": (4096, B), "SC": (4096, B), "MP": (256, B),
-    "WE": (1792, B), "WO": (1792, F), "WO2": (1792, F), "WOB": (1536, B),
+    "WE": (1792, B), "WE2": (1792, B), "WO": (1792, F), "WO2": (1792, F), "WOB": (1536, B),
     "AW": (96, B), "PL": (96, B), "PA": (96, F), "PB": (96, F), "PC": (96, F), "OF16": (96, U), "A1": (96, B),
     "REST": (96, B), "YWF": (96, F), "YCF": (192, F), "YCI": (192, I),
     "Q": (256, F), "S": (16 * 20, F), "WN": (16, B), "WP": (16, B),
@@ -33,11 +37,11 @@ _SB = {
     "H": (256, F), "TT": (256, F), "TB16": (256, U),
     "IP": (192, B), "IH": (192, F), "IT": (192, F), "TI16": (192, U), "IS": (192, B),
     "GO_": (256, B), "GK": (256, B), "K": (800, B), "KD": (32, B),
-    "LW": (64, F), "L16": (4, U), "EQ": (64, F), "EQS": (64, F), "CC": (64, F), "MN": (32, F), "MT": (32, F),
-    "CFL": (32, F), "FL": (32, B), "XS": (32, F), "BAD": (2, F), "X4": (4, F), "X5": (4, F), "AL16": (4 * STEPS, U),
+    "LW": (64, F), "L16": (4, U), "EQ": (64, B), "CC": (64, F), "MN": (32, B), "PEN2": (32, B), "GNN": (128, B),
+    "FL": (32, B), "XS": (32, F), "X4": (4, F), "AL16": (4 * STEPS, U),
     "CN": (32, F), "RV": (32, B), "RF": (32, F), "NEG": (32, B),
-    "EX16": (12, U), "E1": (192, B), "E2": (192, B), "SND": (192 * STEPS, B), "LAND": (192 * STEPS, B),
-    "PI": (8, I), "PC_": (24, F), "IX": (144, F), "IG": (128, F), "IR": (128, F),
+    "EX16": (12, U), "SND": (192 * STEPS, B), "LAND": (192 * STEPS, B),
+    "PI": (8, I), "PC_": (28, F), "IX": (144, F), "IG": (128, F), "IR": (128, F),
     "IDN": (128, B), "ID8": (128, B), "GON": (128, B), "TRI": (128, B), "PKU": (128, B), "PKO": (128, B),
     "P1": (128, B), "P2": (128, B), "BCO": (144, B), "BAL": (144, B), "BE": (144, B), "BO": (144, B), "BF": (144, F),
     "BEF": (144, F), "LC": (128, B), "LY": (128, B), "LT": (128, F), "ZR": (128, B), "R": (4096, B),
@@ -202,7 +206,6 @@ def rank_program(g, core, T, topo):
     dma("s", V("GV"), T.gv[:], 6.5)
     dma("a", V("X0"), T.x0[:], 8.0)
     dma("a", V("EXI"), T.ex[:])
-    dma("a", V("C", OFF, DEF), T.co[:], 12.0)
 
     iota(V("PI", 0, 1), [[0, 1]], 0, 1)
     iota(V("IX"), [[1, 144]], 0, 0)
@@ -213,28 +216,28 @@ def rank_program(g, core, T, topo):
     iota(V("IG"), [[1, 8], [0, 16]], 0, 0)
     dma("s", V("R", p0=0, p1=3), V("ZR", p0=0, p1=96))
     dma("s", V("R", 0, 4096, 1, 3, 5), V("ZR", p0=32, p1=96))
+    add("s", lambda e: e.dma_start(ap(V("C", OFF, DEF)), T.co[:]), [V("C", OFF, DEF)], [V("GV")], kind="d", lat=8.0)
     iota(V("ND", 0, 256), [[0, 256]], 0, 0)
-    iota(V("NA", 0, 256), [[0, 256]], 0, 0)
+    bump[0] = 20.0
+    act(V("NA", 0, 256), V("ND", 0, 256), AF.Silu)
+    bump[0] = 0.0
     iota(V("JT"), [[1, 256]], NG, 0)
     iota(V("STA", 0, 256), [[0, 256]], int(STAMP[0]), 0)
     iota(V("STD", 0, 128), [[0, 128]], int(STAMP[0]), 0)
-    iota(V("MK"), [[0, YW]], 0, 0)
-    iota(V("MK", DEF, DEF + 1), [[0, 1]], 1000000, 0)
     iota(V("WO"), [[0, 1792]], 0, 0)
     iota(V("WE"), [[0, 1792]], 0, 0)
     iota(V("WO2"), [[0, 1792]], 0, 0)
+    iota(V("WE2"), [[0, 1792]], 0, 0)
     mset(V("D0M"), 1.0)
     mset(V("D0S"), 1.0)
     mset(V("CST"), -240.0 * KM)
     mset(V("Y", 0, OFF), 0.0)
     mset(V("C", 0, OFF), EMPTY)
     mset(V("C", DEF, YW), EMPTY)
-    mset(V("S32"), 1.0)
     mset(V("NEG"), -1.0)
     mset(V("D0M", 0, 512, 16), 0.0)
     mset(V("D0S", 0, 256, 16), 0.0)
     mset(V("D0S", 15, 256, 16), 0.0)
-    mset(V("S32", 32, 33), 0.0)
     ts(V("PI", 1, 2), V("PI", 0, 1), 15, ALU.bitwise_and)
     ts(V("PI", 2, 3), V("PI", 0, 1), 4, ALU.arith_shift_right)
     ts(V("PI", 3, 4), V("PI", 0, 1), 5, ALU.arith_shift_right)
@@ -276,16 +279,28 @@ def rank_program(g, core, T, topo):
         mm(V(pk, 0, b - a), V("LC", p1=5), V("R", a, b, p1=5), True, True)
         act(V("CODE", a, b), V(pk, 0, b - a), AF.Copy)
     act(V("Y", IMP, YW), V("CODE", IMP, YW), AF.Copy)
+    mset(V("Y", DEF, DEF + 1), 0.0)
+    mset(V("CODE", 0, 1), 0.0)
+    mset(col(26), BIG)
+    ts(col(24), col(1), 5.0, ALU.is_equal)
+    ts(col(25), col(19), 4096.0, ALU.mult, -4096.0, ALU.add)
+    ts(V("SCF", 0, 8), V("IX", 0, 8), 1.0, ALU.add, col(24), ALU.mult)
+    ts(col(23), col(24), 64.0, ALU.mult, col(19), ALU.subtract)
+    ts(V("SCF", 0, 8), V("SCF", 0, 8), 1.0, ALU.add)
+    ts(V("SCF", 8, 16), V("SCF", 0, 8), col(25), ALU.mult, 2048.0, ALU.add)
 
     def ranks(t):
         if t == 0:
             cp(V("AW"), V("AWI"))
         else:
-            ts(V("AW"), V("ps2", 0, 96), 0.75 * STAMP[t - 1], ALU.is_ge)
+            ts(V("AW"), V("ps2", 0, 96), 0.81 * STAMP[t - 1], ALU.is_ge)
         scan(V("PL"), V("AW"), V("AW"), 0.0, ALU.add, ALU.max)
         mm(V("ps3", 0, 1), V("TRI"), V("PL", 95, 96), True, True)
-        ts(V("PA"), V("AW"), -BIG, ALU.mult, BIG, ALU.add)
-        tt(V("PB"), V("PA"), V("PL"), ALU.add)
+        if t == 0 or not PAA:
+            ts(V("ps7", 288, 384), V("AW"), -BIG, ALU.mult, BIG, ALU.add)
+        else:
+            act(V("ps7", 288, 384), V("AW"), AF.Identity, bias=col(26), scale=-BIG)
+        tt(V("PB"), V("PL"), V("ps7", 288, 384), ALU.add)
         tt(V("PC"), V("PB"), JG, ALU.min)
         ts(V("OF16"), V("PC"), V("ps3", 0, 1), ALU.add, -0.75, ALU.add)
 
@@ -315,14 +330,15 @@ def rank_program(g, core, T, topo):
         ts(V("PKU"), V("GON"), col(14), ALU.mult)
         ts(V("PKO"), V("GON"), col(13), ALU.mult)
         ts(V("PEN", 0, 64), V("IR", 0, 64), col(1), ALU.not_equal, -BIG, ALU.mult)
-        ts(V("PEN", 64, 96), V("IX", 0, 32), col(1), ALU.is_ge, BIG, ALU.mult)
-        ts(V("PT", 32, 64), V("IX", 0, 32), -16.0, ALU.add, col(1), ALU.is_ge)
+        ts(V("PEN", 64, 96), V("IX", 0, 32), col(1), ALU.is_le, BIG, ALU.mult)
+        ts(V("PT", 32, 64), V("IX", 0, 32), -16.0, ALU.add, col(1), ALU.is_le)
+        ts(V("PEN2"), V("PEN", 0, 32), 16.0, ALU.add)
+        ts(V("GNN"), V("GON"), -1.0 / 32768.0, ALU.mult)
         ts(V("SEG"), V("IR", 0, 64), 0.5, ALU.is_lt, -4.0 * BIG, ALU.mult)
         ts(V("PEN", 96, 128), V("PT", 32, 64), BIG, ALU.mult)
         ts(V("JB"), V("IX", 0, 8), 16.0, ALU.mult, col(1), ALU.add)
         ts(V("KD", 0, 1), V("CODE", DEF, DEF + 1), col(15), ALU.mult, col(16), ALU.add)
-        ts(V("DJ", 0, 2), V("JB", 0, 2), float(DMP), ALU.add)
-        ts(V("DJ", 2, 4), V("JB", 0, 2), float(DMP), ALU.add)
+        ts(V("DJ", 0, 2), V("JB", 0, 2), DMP + 0.25, ALU.add)
         tt(col(22), V("KD", 0, 1), V("CODE", DEF, DEF + 1), ALU.max)
         ts(V("JB"), V("JB"), float(NG), ALU.add)
         ts(V("EX16"), V("EXI"), OFF + 0.25, ALU.add)
@@ -331,7 +347,6 @@ def rank_program(g, core, T, topo):
         ts(V("P2"), V("IX", 0, 128), col(18), ALU.is_equal)
 
     def wake_constants():
-        cp(CIMP, V("CODE", IMP, DEF))
         ts(V("BE"), V("IX"), col(20), ALU.is_equal, col(19), ALU.mult)
         ts(V("BEF"), V("IX"), col(20), ALU.is_equal, col(19), ALU.mult)
         ts(V("BO"), V("IX"), col(21), ALU.is_equal, col(19), ALU.mult)
@@ -368,39 +383,44 @@ def rank_program(g, core, T, topo):
 
     for t in range(STEPS):
         std, sta = V("STD", 128 * t, 128 * t + 128), V("STA", 256 * t, 256 * t + 256)
-        ct = "C" if t == 0 else "CF"
+        ct = "C"
         rows = list(range(KA[t], 16))
 
         def wake_row(rows=rows, std=std):
             if rows:
                 r = rows.pop(0)
-                cp(X(V("WE"), V("TB16", 8 * r, 8 * r + 8)), std)
+                cp(X(V("WE2" if r % 2 else "WE"), V("TB16", 8 * r, 8 * r + 8)), std)
 
         dq = DQ[t]
-        for a, b in ((16 * dq, 16 * dq + 64), (0, 16 * dq), (16 * dq + 64, 256)):
-            tt(V("NM", a, b), V("ND", a, b), V("NA", a, b), ALU.max)
+        for a, b in ((16 * dq, 256), (0, 16 * dq)) if NM2 else ((16 * dq, 16 * dq + 64), (0, 16 * dq), (16 * dq + 64, 256)):
+            if NMP and b - a > 64:
+                act(V("ps6", a, b), V("NA", a, b), AF.Copy)
+                tt(V("NM", a, b), V("ND", a, b), V("ps6", a, b), ALU.max)
+            else:
+                tt(V("NM", a, b), V("ND", a, b), V("NA", a, b), ALU.max)
             bump[1] = 3.0
             ts(V("N16", a, b), V("NM", a, b), 0.25, ALU.add)
             bump[1] = 0.0
         if t + 1 < STEPS:
             iota(V("ND", 0, 256), [[0, 256]], 0, 0)
             iota(V("NA", 0, 256), [[0, 256]], 0, 0)
-        for q in range(0, 16, 2):
-            src = X(V("Y"), V("N16", 16 * q, 16 * q + 32))
+        cuts = [(q, min(q + 2, dq)) for q in range(0, dq, 2)] + [(q, min(q + 2, 16)) for q in range(dq, 16, 2)]
+        for q, q2 in cuts:
+            src = X(V("Y"), V("N16", 16 * q, 16 * q2))
             if q < dq:
-                cp(V("G", 256 * q, 256 * q + 512), src)
+                cp(V("G", 256 * q, 256 * q2), src)
             else:
-                act(V("G", 256 * q, 256 * q + 512), src, AF.Copy)
+                act(V("G", 256 * q, 256 * q2), src, AF.Copy)
         mm(V("ps1", 0, 16), V("IDN"), V("CST"), True, False)
-        for q in range(0, 16, 2):
-            scan(V("SC", 256 * q, 256 * q + 512), V("D0M"), V("G", 256 * q, 256 * q + 512), 0.0, ALU.mult, ALU.max)
+        for q, q2 in cuts:
+            scan(V("SC", 256 * q, 256 * q2), V("D0M", 0, 256 * (q2 - q)), V("G", 256 * q, 256 * q2), 0.0, ALU.mult,
+                 ALU.max)
         order = sorted(range(16), key=lambda q: (q // 2 + 0.5 if q < dq else (q - dq) // 2, q))
         for n, q in enumerate(order):
             mm(V("ps0", 0, 256), V("BCO", 15 - q, 143 - q), V("G", 256 * q, 256 * q + 256), n == 0, n == 15)
         for q in range(16):
             mm(V("ps1", 0, 16), V("BAL", 15 - q, 143 - q), V("SC", 256 * q + 14, 256 * q + 256, 16), False, q == 15)
-        act(V("MP"), X(V("SC"), V("LM16")), AF.Copy)
-        ts(V("A1"), V("PL"), V("ps3", 0, 1), ALU.add, 256.5, ALU.is_gt)
+        ts(V("ps5", 384, 480), V("PL"), V("ps3", 0, 1), ALU.add, 256.5, ALU.is_gt)
         bump[0] = BA
         if t == 0:
             for k in range(4):
@@ -408,7 +428,7 @@ def rank_program(g, core, T, topo):
                    ALU.bitwise_and)
         bump[0] = 0.0
         bump[1] = 6.0
-        tt(V("REST"), V("A1"), V("AW"), ALU.mult)
+        tt(V("REST"), V("AW"), V("ps5", 384, 480), ALU.mult)
         bump[1] = 0.0
         scan(V("Q"), V("D0S"), V("ps0", 0, 256), 0.0, ALU.mult, ALU.add)
         Sn, So = V("Q", 14, 256, 16), V("Q", 15, 256, 16)
@@ -433,10 +453,18 @@ def rank_program(g, core, T, topo):
         tt(S_(12), V("WN"), Sn, ALU.mult)
         ts(V("BW16"), S_(11), 0.25 - CB, ALU.add)
         bump[1] = BT
-        ts(V("TB16"), X(V("TT"), V("LR16")), 0.25, ALU.add)
+        ts(V("TB16", 128, 160), X(V("TT"), V("LR16", 8, 10)), 0.25, ALU.add)
+        bump[1] = BT2
+        ts(V("TB16", 0, 128), X(V("TT"), V("LR16", 0, 8)), 0.25, ALU.add)
+        ts(V("TB16", 160, 256), X(V("TT"), V("LR16", 10, 16)), 0.25, ALU.add)
         bump[1] = 0.0
-        act(V("GO_"), X(V("CODE"), V("BW16")), AF.Identity, bias=col(16), scale=col(15))
-        act(X(V("MK"), V("BW16")), sta, AF.Silu)
+        ts(V("OW16"), S_(10), 0.25 - CB, ALU.add)
+        act(V("OWG"), X(V("CODE"), V("OW16")), AF.Identity, bias=0.0, scale=V("SCF", t, t + 1))
+        act(V("GO_"), V("OWG"), AF.Identity, bias=col(16), scale=col(15))
+        act(V("MPA"), X(V("SC"), V("LM16")), AF.Copy)
+        mm(V("ps7", 0, 256), V("IDN"), V("MPA"), True, False)
+        mm(V("ps7", 0, 256), V("IDN"), V("OWG"), False, True)
+        act(V("MP"), V("ps7", 0, 256), AF.Copy)
         for r in range(16, 32):
             bump[0] = -0.6 * min(r - 16, KA[t])
             act(X(V("WO"), V("TB16", 8 * r, 8 * r + 8)), V("STA", 256 * t, 256 * t + 128), AF.Silu)
@@ -459,42 +487,34 @@ def rank_program(g, core, T, topo):
         mm(V("ps4", 32, 64), V("PKO"), V("K", 0, 32), False, False)
         mm(V("ps4", 64, 96), V("PKU"), V("K", 0, 32), False, False)
         mm(V("ps4", 96, 128), V("PKU"), V("K", 0, 32), False, True)
-        cp(X(V("Y"), V("OB16")), V("MP"))
+        cp(X(V("Y"), V("BW16")), V("MP"))
         scan(V("LW"), V("SEG"), V("ps4", 0, 64), 0.0, ALU.add, ALU.max)
         ts(V("L16"), V("LW", 15, 64, 16), 0.25 - 65.0, ALU.add)
         ts(V("EQ", 0, 32), V("ps4", 64, 96), V("LW", 15, 16), ALU.is_equal)
         ts(V("EQ", 32, 64), V("ps4", 96, 128), V("LW", 31, 32), ALU.is_equal)
         cp(V("CC"), X(V(ct), V("L16")))
-        ts(V("MT"), X(V("MK"), V("L16", 0, 2)), -0.75 * STAMP[t], ALU.add, -10000.0, ALU.mult)
+        ts(V("FL"), X(V("Y"), V("L16", 0, 2)), col(23), ALU.mult, V("SCF", 8 + t, 9 + t), ALU.is_lt)
         tt(V("MN"), V("CC", 0, 32), V("CC", 32, 64), ALU.max)
-        scan(V("EQS"), V("S32"), V("EQ"), 0.0, ALU.mult, ALU.max)
-        tt(V("CFL"), V("MN"), V("MT"), ALU.min)
         tt(V("CN"), V("CC", 0, 32), V("CC", 32, 64), ALU.min)
-        ts(V("FL"), V("CFL"), 2048.0, ALU.is_lt)
-        mm(V("ps3", 0, 32), V("IDN"), V("PEN", 0, 32), True, False)
-        mm(V("ps3", 0, 32), V("GON"), V("FL"), False, True)
+        mm(V("ps3", 0, 32), V("IDN"), V("PEN2"), True, False)
+        mm(V("ps3", 0, 32), V("GON"), V("EQ", 0, 32), False, False)
+        mm(V("ps3", 0, 32), V("GON"), V("EQ", 32, 64), False, False)
+        mm(V("ps3", 0, 32), V("GON"), V("FL"), False, False)
+        mm(V("ps3", 0, 32), V("GNN"), V("MN"), False, True)
         wake_row()
         scan(V("XS"), V("SEG", 0, 32), V("ps3", 0, 32), 0.0, ALU.add, ALU.max)
-        tt(V("BAD"), V("XS", 15, 32, 16), V("EQS", 31, 64, 32), ALU.max)
-        ts(V("BAD"), V("BAD"), BIG, ALU.mult, -65.0, ALU.add)
-        tt(V("X4", 0, 2), V("LW", 15, 32, 16), V("BAD"), ALU.add)
-        tt(V("X4", 2, 4), V("LW", 47, 64, 16), V("BAD"), ALU.add)
-        tt(V("X5"), V("X4"), V("DJ"), ALU.min)
-        ts(V("AL16", 4 * t, 4 * t + 4), V("X5"), 0.25, ALU.add)
+        ts(V("X4", 0, 2), V("XS", 15, 32, 16), BIG, ALU.mult, 0.25 - 65.0, ALU.add)
+        for b in range(2):
+            ts(V("AL16", 4 * t + b, 4 * t + 4, 2), V("LW", 15 + 16 * b, 64, 32), V("X4", b, b + 1), ALU.add,
+               V("DJ", b, b + 1), ALU.min)
         refresh("Y", "RV", t, lambda: None)
-        cp(V("E1"), X(V("Y"), V("EX16")))
-        bump[0] = 4.0 if t + 1 == STEPS else 0.0
-        cp(X(V(ct), V("AL16", 4 * t, 4 * t + 2)), V("CN"))
-        bump[0] = 0.0
-        ts(V("E2"), V("E1"), KM, ALU.mult, 0.0, ALU.min)
-        for d in range(1, N):
-            pm = V(("IDN", "P1", "P2")[d % 3])
-            a = NE * (d - 1)
-            mm(V("ps6", a, a + NE), pm, V("E1", a, a + NE), True, False)
-            mm(V("ps6", a, a + NE), pm, V("E2", a, a + NE), False, True)
-        wake_row()
-        cp(V("SND", 192 * t, 192 * t + 192), V("ps6", 0, 192))
+        cp(V("SND", 192 * t, 192 * t + 192), X(V("Y"), V("EX16")))
         send(t)
+        cp(X(V("C"), V("AL16", 4 * t, 4 * t + 2)), V("CN"))
+        if t > 0:
+            bump[0] = 4.0 if t + 1 == STEPS else 0.0
+            cp(X(V("CF"), V("AL16", 4 * t, 4 * t + 2)), V("CN"))
+            bump[0] = 0.0
         if t == 0:
             for k in range(1, STEPS):
                 iota(V("STA", 256 * k, 256 * k + 256), [[0, 256]], int(STAMP[k]), 0)
@@ -509,6 +529,7 @@ def rank_program(g, core, T, topo):
             for a, b in ((0, 1440), (1440, NV)):
                 ts(V("YO", a, b), V("Y", OFF + a, OFF + b), -1.0, ALU.max)
                 dma("s", T.yx[:, a:b], V("YO", a, b), 2.5)
+            bump[0] = BFT
             refresh("FT", "RF", t, lambda: None)
             dma("s", T.yf[:], V("FT", OFF, DEF, p0=0, p1=128, ps=16), 2.5)
             bump[0] = 0.0
@@ -517,16 +538,21 @@ def rank_program(g, core, T, topo):
         while len(rows) > 3:
             wake_row()
         land = V("LAND", 192 * t, 192 * t + 192)
-        add("v", lambda e, land=land: e.tensor_scalar(ap(V("IS")), ap(land), -1.0, 0.0, ALU.mult, ALU.max), [V("IS")], [],
+        add("v", lambda e, land=land: e.tensor_scalar(ap(V("IS")), ap(land), KM, 0.0, ALU.mult, ALU.min), [V("IS")], [],
             ext=("arr%d" % t, n_arr))
-        mm(V("ps6", 0, 192), V("IDN"), V("IS"), True, t == 0)
-        if t > 0:
-            mm(V("ps6", 0, 192), V("IDN"), V("IP"), False, True)
+        for d in range(1, N):
+            pm, a = V(("IDN", "P1", "P2")[d % 3]), NE * (d - 1)
+            mm(V("ps6", a, a + NE), pm, V("IS", a, a + NE), True, t == 0)
+            if t > 0:
+                mm(V("ps6", a, a + NE), pm, V("IP", a, a + NE), False, True)
+        for d in range(1, N):
+            pm, a = V(("IDN", "P1", "P2")[d % 3]), NE * (d - 1)
+            mm(V("ps4", 128 + a, 128 + a + NE), pm, V("IS", a, a + NE), True, False)
+            mm(V("ps4", 128 + a, 128 + a + NE), pm, V("LAND", 192 * t + a, 192 * t + a + NE), False, True)
         if t + 1 < STEPS:
-            add("v", lambda e, land=land: e.tensor_tensor(ap(V("Y", IMP, DEF)), ap(land), ap(CIMP), ALU.max),
-                [V("Y", IMP, DEF)], [land, CIMP, V("IS")])
+            tt(V("Y", IMP, DEF), V("CODE", IMP, DEF), V("ps4", 128, 320), ALU.max)
         wake_row()
-        tt(V("IH"), V(ct, IMP, DEF), V("ps6", 0, 192), ALU.add)
+        tt(V("IH"), V(ct, IMP, DEF), V("ps6", 0, 192), ALU.subtract)
         wake_row()
         trn(V("IT"), V("IH"))
         wake_row()
@@ -541,13 +567,13 @@ def rank_program(g, core, T, topo):
         def import_row(irows=irows, t=t):
             if irows:
                 r = irows.pop(0)
-                cp(X(V("WE"), V("TI16", 6 * r, 6 * r + 6)), V("STD", 128 * t, 128 * t + 96))
+                cp(X(V("WE2" if r % 2 and r < W2L else "WE"), V("TI16", 6 * r, 6 * r + 6)), V("STD", 128 * t, 128 * t + 96))
 
         if t + 1 < STEPS:
-            ts(V("IP"), land, 0.0, ALU.is_ge, BIG, ALU.mult, after=[V("IS")])
+            ts(V("IP"), land, 0.0, ALU.is_ge, -BIG, ALU.mult, after=[V("IS")])
             refresh("Y", "RV", t, import_row)
         else:
-            ts(V("YO", NV, 3072), land, -1.0, ALU.max, after=[V("IS")])
+            ts(V("YO", NV, 3072), V("ps4", 128, 320), -1.0, ALU.max)
             dma("s", T.yx[:, NV:3072], V("YO", NV, 3072), 2.5)
             ts(V("YCI"), V("ps7", 0, 192), 16.0, ALU.add)
             ts(V("YCI"), V("YCI"), EMPTY, ALU.bitwise_and)
@@ -559,18 +585,20 @@ def rank_program(g, core, T, topo):
         if KA[t]:
             for q in range(16):
                 mm(V("ps2", 0, 96), V("BEF", 15 - q, 143 - q), V("WO2", 96 * q, 96 * q + 96), False, False)
+        for q in range(16):
+            mm(V("ps2", 0, 96), V("BE", 15 - q, 143 - q), V("WE2", 96 * q, 96 * q + 96), False, False)
         two = [("BO", "WOB"), ("BE", "WE")]
         for n, (sel, win) in enumerate(two[::-1] if EVEN_FIRST else two):
             for q in range(16):
                 mm(V("ps2", 0, 96), V(sel, 15 - q, 143 - q), V(win, 96 * q, 96 * q + 96), False, n == 1 and q == 15)
-        if t == 0:
-            for k in range(8):
-                cp(V("CF", 424 * k, 424 * k + 424), V("C", 424 * k, 424 * k + 424))
+        for k in range(CFK[t], CFK[t + 1]):
+            bump[0] = 0.0
+            cp(V("CF", OFF + 384 * k, OFF + 384 * k + 384), V("C", OFF + 384 * k, OFF + 384 * k + 384))
         if t + 1 < STEPS:
             ranks(t + 1)
             compaction(t + 1)
         else:
-            ts(V("YWF"), V("ps2", 0, 96), 0.75 * STAMP[t], ALU.is_ge)
+            ts(V("YWF"), V("ps2", 0, 96), 0.81 * STAMP[t], ALU.is_ge)
             dma("s", T.yw[:], V("YWF"), 2.5)
 
     n_ops = len(ops)

from concourse.bass import DstId, RemoteDMATransfer
from concourse.mybir import AluOpType as ALU, ActivationFunctionType as AF

NV, NE, NG, STEPS = 2880, 64, 1536, 5
OFF = 256
IMP = OFF + NV
DEF = OFF + 3072
DMP = DEF + 2
YW = 3392
CB = 4161.0
KM = 8192.0
BIG = 16384.0
EMPTY = 32767
STAMP = [2.0 * 8 ** t for t in range(STEPS)]
DQ = [1, 6, 6, 6, 6]
DC = [20, 48, 50, 50, 46]
KA = [5, 5, 5, 5, 7]
EVEN_FIRST = True
W2L = 12
PAA, NMP = True, True
BT2, NM2, BFT = 3.0, False, 0.0
CFK = [0, 3, 6, 8, 8, 8]
B2, BT, BL, BA = 15.0, 6.0, 8.0, 0.0
CY, PE_CY, SEM, ARRIVE, LOOK, GATH, SCAT = 1.04e-3, 0.8e-3, 0.06, 4.5, 0.09, 1.56, 3.8

F, B, I, U = "float32", "bfloat16", "int32", "uint16"
_SB = {
    "X0": (NV, B), "GV": (NG, I), "C": (YW, I), "AWI": (96, I), "EXI": (12, I),
    "Y": (YW, B), "CODE": (YW, B), "OWG": (256, B), "MPA": (256, B), "OW16": (16, U), "SCF": (16, F), "FT": (YW, F), "CF": (YW, F), "YO": (3072, B),
    "GVP": (NG, F), "ND": (4640, F), "NA": (4640, F), "NM": (256, F), "N16": (256, U),
    "G": (4096, B), "SC": (4096, B), "MP": (256, B),
    "WE": (1792, B), "WE2": (1792, B), "WO": (1792, F), "WO2": (1792, F), "WOB": (1536, B),
    "AW": (96, B), "PL": (96, B), "PA": (96, F), "PB": (96, F), "PC": (96, F), "OF16": (96, U), "A1": (96, B),
    "REST": (96, B), "YWF": (96, F), "YCF": (192, F), "YCI": (192, I),
    "Q": (256, F), "S": (16 * 20, F), "WN": (16, B), "WP": (16, B),
    "OB16": (16, U), "BW16": (16, U), "UL16": (16, U), "KO16": (16, U),
    "H": (256, F), "TT": (256, F), "TB16": (256, U),
    "IP": (192, B), "IH": (192, F), "IT": (192, F), "TI16": (192, U), "IS": (192, B),
    "GO_": (256, B), "GK": (256, B), "K": (800, B), "KD": (32, B),
    "LW": (64, F), "L16": (4, U), "EQ": (64, B), "CC": (64, F), "MN": (32, B), "PEN2": (32, B), "GNN": (128, B),
    "FL": (32, B), "XS": (32, F), "X4": (4, F), "AL16": (4 * STEPS, U),
    "CN": (32, F), "RV": (32, B), "RF": (32, F), "NEG": (32, B),
    "EX16": (12, U), "SND": (192 * STEPS, B), "LAND": (192 * STEPS, B),
    "PI": (8, I), "PC_": (28, F), "IX": (144, F), "IG": (128, F), "IR": (128, F),
    "IDN": (128, B), "ID8": (128, B), "GON": (128, B), "TRI": (128, B), "PKU": (128, B), "PKO": (128, B),
    "P1": (128, B), "P2": (128, B), "BCO": (144, B), "BAL": (144, B), "BE": (144, B), "BO": (144, B), "BF": (144, F),
    "BEF": (144, F), "LC": (128, B), "LY": (128, B), "LT": (128, F), "ZR": (128, B), "R": (4096, B),
    "D0M": (512, B), "D0S": (256, B), "SEG": (64, F), "S32": (64, F), "PEN": (128, B), "PT": (128, F),
    "CST": (16, B), "J16": (16, F), "JK": (16, F), "JT": (256, F), "DJ": (4, F), "JB": (8, F),
    "LM16": (16, U), "LR16": (16, U),
    "STD": (128 * STEPS, B), "STA": (256 * STEPS, F),
}
SCRATCH = {k: ("sbuf", [128, n], d) for k, (n, d) in _SB.items()}
for _k in range(8):
    SCRATCH["ps%d" % _k] = ("psum", [128, 512], F)
NDMA = 24
SEMAPHORES = ["qv", "qa", "qt", "qg", "sent"] + ["dm%d" % k for k in range(NDMA)] + ["arr%d" % t for t in range(STEPS)]


def V(name, a=0, b=None, s=1, p0=0, p1=128, ps=1):
    if b is None:
        b = SCRATCH[name][1][1]
    return ("v", name, a, b, s, p0, p1, ps)


def X(win, off):
    return ("x", win, off)


def rank_program(g, core, T, topo):
    rank = T.rank_of(core)
    if rank is None:
        return
    cores = list(T.cores)
    N = len(cores)
    eng = {"v": g.vector, "a": g.scalar, "t": g.tensor, "g": g, "s": g.sync}
    ops = []
    hist = {}
    ndma, pool, prev, sends, bump = [0], [], {}, [], [0.0, 0.0]

    def ap(x):
        if not isinstance(x, tuple):
            return x
        if x[0] == "x":
            return ap(x[1]).indirect(ap(x[2]))
        return T[x[1]][x[5]:x[6]:x[7], x[2]:x[3]:x[4]] if (x[4] != 1 or x[7] != 1) else T[x[1]][x[5]:x[6], x[2]:x[3]]

    def width(x):
        return 16 * (x[2][3] - x[2][2]) if x[0] == "x" else len(range(x[2], x[3], x[4]))

    def cost(q, outs, ins, kind, per):
        if kind != "c":
            return 0.1 if kind == "d" else 0.5
        aps = [x for x in outs + ins if isinstance(x, tuple)]
        n = width(outs[0])
        if q == "t":
            return max(64, n) * (4 if SCRATCH[ins[0][1]][2] == F else 1) * PE_CY
        if q == "g":
            return 0.16 + 2 * n * CY
        if outs[0][0] == "x":
            return 0.07 + SCAT * n * CY
        if ins and ins[0][0] == "x":
            return 0.07 + GATH * n * CY
        if per == 2 and any(x[1].startswith("ps") for x in aps[1:]):
            per = 1
        if per == 1 and q == "v" and all(SCRATCH[x[1]][2] in (B, U) for x in aps if width(x) > 1):
            per = 0.5
        return max(64, n * per) * CY

    def add(q, emit, outs, ins, kind="c", ext=None, per=1, lat=0.0):
        acc = []
        for lst, w in ((outs, True), (ins, False)):
            for x in lst:
                if not isinstance(x, tuple):
                    continue
                if x[0] == "x":
                    acc.append((x[1], w, False))
                    acc.append((x[2], False, False))
                else:
                    acc.append((x, w, w))
        i = len(ops)
        deps, order = set(), set()
        for x, w, _ in acc:
            name, lo, hi = x[1], x[2], x[3]
            bank = name.startswith("ps")
            for (l2, h2, j, w2, pa, pb, s2) in hist.get(name, []):
                same = ops[j][0] == q and ops[j][3] == "c" and kind == "c"
                if bank and same and q == "t":
                    order.add(j)
                elif bank and not same:
                    deps.add(j)
                elif l2 < hi and lo < h2 and (w or w2) and pa < x[6] and x[5] < pb:
                    if s2 > 1 and s2 == x[4] and (lo - l2) % s2:
                        continue
                    if not same or q != "t":
                        deps.add(j)
        for x, w, whole in acc:
            h = hist.setdefault(x[1], [])
            if w and x[4] == 1 and x[5] == 0 and x[6] == 128 and x[7] == 1:
                h[:] = [e for e in h if not (x[2] <= e[0] and e[1] <= x[3] and (e[2] in deps or e[2] in order))]
            h.append((x[2], x[3], i, w, x[5], x[6], x[4]))
        if q == "g" and kind == "c":
            if pool:
                deps.add(pool[-1])
            pool.append(i)
        if q == "g" or (kind == "d" and lat != 2.5):
            if q in prev:
                order.add(prev[q])
            prev[q] = i
        if ext is not None:
            order.add(sends[-1])
        if kind == "r":
            sends.append(i)
            lat = ARRIVE
        ops.append([q, emit, deps, kind, False, ext, order, cost(q, outs, ins, kind, per), lat, bump[0], bump[1]])
        return i

    def cp(out, in_):
        add("v", lambda e: e.tensor_copy(ap(out), ap(in_)), [out], [in_])

    def tt(out, a, b, op):
        add("v", lambda e: e.tensor_tensor(ap(out), ap(a), ap(b), op), [out], [a, b], per=2)

    def ts(out, a, s1, op0, s2=None, op1=None, after=()):
        if op1 is None:
            add("v", lambda e: e.tensor_scalar(ap(out), ap(a), ap(s1), None, op0), [out], [a, s1] + list(after))
        else:
            add("v", lambda e: e.tensor_scalar(ap(out), ap(a), ap(s1), ap(s2), op0, op1), [out], [a, s1, s2] + list(after))

    def scan(out, d0, d1, init, op0, op1):
        add("v", lambda e: e.tensor_tensor_scan(ap(out), ap(d0), ap(d1), init, op0, op1), [out], [d0, d1])

    def trn(out, in_):
        add("v", lambda e: e.transpose(ap(out), ap(in_)), [out], [in_])

    def mset(out, c):
        add("v", lambda e: e.memset(ap(out), c), [out], [])

    def act(out, in_, func, bias=None, scale=None):
        if bias is None:
            add("a", lambda e: e.activation(ap(out), ap(in_), func), [out], [in_])
        else:
            add("a", lambda e: e.activation(ap(out), ap(in_), func, bias=ap(bias), scale=ap(scale)), [out], [in_, bias, scale])

    def mm(out, lhsT, rhs, start, stop):
        add("t", lambda e: e.matmul(ap(out), ap(lhsT), ap(rhs), start, stop), [out], [lhsT, rhs])

    def iota(out, pat, base, ch):
        if SCRATCH[out[1]][2] == I:
            add("g", lambda e: e.iota(ap(out), pat, base, ch), [out], [])
        else:
            add("g", lambda e: e.iota(ap(out), pat, base, ch, allow_small_or_imprecise_dtypes=True), [out], [])

    def dma(q, out, in_, lat=2.2):
        add(q, lambda e: e.dma_start(ap(out), ap(in_)), [out], [in_], kind="d", lat=lat)

    def col(k):
        return V("PC_", k, k + 1)

    def S_(k):
        return V("S", 16 * k, 16 * k + 16)

    CIMP, JG = V("ps5", 0, 192), V("ps5", 192, 288)

    dma("s", V("AWI"), T.aw[:])
    dma("s", V("GV"), T.gv[:], 6.5)
    dma("a", V("X0"), T.x0[:], 8.0)
    dma("a", V("EXI"), T.ex[:])

    iota(V("PI", 0, 1), [[0, 1]], 0, 1)
    iota(V("IX"), [[1, 144]], 0, 0)
    mset(V("ZR", p0=0, p1=32), 1.0)
    iota(V("ZR", p0=32, p1=64), [[-64, 2], [0, 64]], -64, -128)
    iota(V("ZR", p0=64, p1=96), [[0, 2], [-1, 64]], -1, 0)
    iota(V("IR"), [[0, 8], [1, 16]], 0, 0)
    iota(V("IG"), [[1, 8], [0, 16]], 0, 0)
    dma("s", V("R", p0=0, p1=3), V("ZR", p0=0, p1=96))
    dma("s", V("R", 0, 4096, 1, 3, 5), V("ZR", p0=32, p1=96))
    add("s", lambda e: e.dma_start(ap(V("C", OFF, DEF)), T.co[:]), [V("C", OFF, DEF)], [V("GV")], kind="d", lat=8.0)
    iota(V("ND", 0, 256), [[0, 256]], 0, 0)
    bump[0] = 20.0
    act(V("NA", 0, 256), V("ND", 0, 256), AF.Silu)
    bump[0] = 0.0
    iota(V("JT"), [[1, 256]], NG, 0)
    iota(V("STA", 0, 256), [[0, 256]], int(STAMP[0]), 0)
    iota(V("STD", 0, 128), [[0, 128]], int(STAMP[0]), 0)
    iota(V("WO"), [[0, 1792]], 0, 0)
    iota(V("WE"), [[0, 1792]], 0, 0)
    iota(V("WO2"), [[0, 1792]], 0, 0)
    iota(V("WE2"), [[0, 1792]], 0, 0)
    mset(V("D0M"), 1.0)
    mset(V("D0S"), 1.0)
    mset(V("CST"), -240.0 * KM)
    mset(V("Y", 0, OFF), 0.0)
    mset(V("C", 0, OFF), EMPTY)
    mset(V("C", DEF, YW), EMPTY)
    mset(V("NEG"), -1.0)
    mset(V("D0M", 0, 512, 16), 0.0)
    mset(V("D0S", 0, 256, 16), 0.0)
    mset(V("D0S", 15, 256, 16), 0.0)
    ts(V("PI", 1, 2), V("PI", 0, 1), 15, ALU.bitwise_and)
    ts(V("PI", 2, 3), V("PI", 0, 1), 4, ALU.arith_shift_right)
    ts(V("PI", 3, 4), V("PI", 0, 1), 5, ALU.arith_shift_right)
    ts(V("PI", 4, 5), V("PI", 0, 1), 7, ALU.bitwise_and)
    cp(V("PC_", 0, 5), V("PI", 0, 5))
    ts(col(5), col(1), 96.0, ALU.mult, 1536.0, ALU.add)
    ts(col(6), col(2), 16.0, ALU.mult, 15.0, ALU.add)
    ts(col(7), col(1), 2.5, ALU.is_lt)
    ts(col(8), col(1), 16.0, ALU.mult, CB, ALU.add)
    ts(col(9), col(1), 256.0, ALU.mult, 14.25, ALU.add)
    ts(col(10), col(1), 7.5, ALU.is_gt, 0.25, ALU.add)
    ts(col(17), col(2), -16.0, ALU.mult, 112.0, ALU.add)
    ts(col(19), col(1), 0.5, ALU.is_lt)
    ts(col(20), col(3), 32.0, ALU.mult, 15.0, ALU.add)
    ts(col(21), col(3), 32.0, ALU.mult, 31.0, ALU.add)
    ts(col(11), col(4), 32.0, ALU.mult, col(10), ALU.add)
    ts(col(12), col(1), 0.5, ALU.is_gt, col(7), ALU.mult)
    ts(col(13), col(1), 4.5, ALU.is_lt, col(7), ALU.subtract)
    tt(col(17), col(17), col(1), ALU.add)
    ts(V("ID8"), V("IX", 0, 128), col(0), ALU.is_equal, KM, ALU.mult)
    ts(col(14), col(12), -1.0, ALU.mult)
    ts(col(15), col(13), -1.0, ALU.mult)
    ts(col(16), col(12), -BIG, ALU.mult)
    ts(col(18), col(17), 111.5, ALU.is_gt, -128.0, ALU.mult)
    ts(V("LT"), V("IX", 0, 128), col(0), ALU.is_gt)
    ts(col(18), col(18), col(17), ALU.add, 16.0, ALU.add)
    ts(V("LC", p1=32), V("IR", p1=32), V("PC_", 0, 1, p1=32), ALU.is_equal)
    ts(V("H", 0, 128, p1=1), V("IR", p1=1), 4.5, ALU.is_gt, -64.0, ALU.mult)
    ts(V("PT", p1=1), V("IR", p1=1), 0.5, ALU.is_lt, -4096.0, ALU.mult)
    ts(JG, V("IX", 0, 96), col(5), ALU.add)
    tt(V("LC", p1=1), V("H", 0, 128, p1=1), V("PT", p1=1), ALU.add)
    ts(V("GON"), V("IG"), col(2), ALU.is_equal)
    cp(V("LY", p1=32), V("LC", p1=32))
    tt(V("TRI"), V("LT"), V("GON"), ALU.mult)
    ts(V("LY", p1=1), V("LC", p1=1), KM, ALU.add)
    for k in range(7):
        a, b = 512 * k, min(512 * k + 512, YW)
        pk = ("ps0", "ps1", "ps2")[k % 3]
        mm(V(pk, 0, b - a), V("LC", p1=5), V("R", a, b, p1=5), True, True)
        act(V("CODE", a, b), V(pk, 0, b - a), AF.Copy)
    act(V("Y", IMP, YW), V("CODE", IMP, YW), AF.Copy)
    mset(V("Y", DEF, DEF + 1), 0.0)
    mset(V("CODE", 0, 1), 0.0)
    mset(col(26), BIG)
    ts(col(24), col(1), 5.0, ALU.is_equal)
    ts(col(25), col(19), 4096.0, ALU.mult, -4096.0, ALU.add)
    ts(V("SCF", 0, 8), V("IX", 0, 8), 1.0, ALU.add, col(24), ALU.mult)
    ts(col(23), col(24), 64.0, ALU.mult, col(19), ALU.subtract)
    ts(V("SCF", 0, 8), V("SCF", 0, 8), 1.0, ALU.add)
    ts(V("SCF", 8, 16), V("SCF", 0, 8), col(25), ALU.mult, 2048.0, ALU.add)

    def ranks(t):
        if t == 0:
            cp(V("AW"), V("AWI"))
        else:
            ts(V("AW"), V("ps2", 0, 96), 0.81 * STAMP[t - 1], ALU.is_ge)
        scan(V("PL"), V("AW"), V("AW"), 0.0, ALU.add, ALU.max)
        mm(V("ps3", 0, 1), V("TRI"), V("PL", 95, 96), True, True)
        if t == 0 or not PAA:
            ts(V("ps7", 288, 384), V("AW"), -BIG, ALU.mult, BIG, ALU.add)
        else:
            act(V("ps7", 288, 384), V("AW"), AF.Identity, bias=col(26), scale=-BIG)
        tt(V("PB"), V("PL"), V("ps7", 288, 384), ALU.add)
        tt(V("PC"), V("PB"), JG, ALU.min)
        ts(V("OF16"), V("PC"), V("ps3", 0, 1), ALU.add, -0.75, ALU.add)

    def compaction(t):
        act(X(V("NA"), V("OF16", DC[t], 96)), V("GVP", 16 * DC[t], NG), AF.Silu)
        cp(X(V("ND"), V("OF16", 0, DC[t])), V("GVP", 0, 16 * DC[t]))

    ranks(0)
    ts(V("IDN"), V("IX", 0, 128), col(0), ALU.is_equal)
    ts(V("BCO"), V("IX"), col(6), ALU.is_equal, col(7), ALU.mult)
    ts(V("BAL"), V("IX"), col(6), ALU.is_equal, KM, ALU.mult)
    ts(V("J16"), V("IX", 0, 16), col(8), ALU.add)
    ts(V("LM16"), V("IX", 0, 16), 16.0, ALU.mult, col(9), ALU.add)
    ts(V("LR16"), V("IX", 0, 16), 2.0, ALU.mult, col(11), ALU.add)
    ts(V("JK"), V("J16"), 300.0 - CB, ALU.add)
    for q in range(16):
        ts(V("GVP", q, NG, 16), V("GV", 96 * q, 96 * q + 96), float(OFF), ALU.add)
    compaction(0)
    for k in range(6):
        a, b = 480 * k, 480 * k + 480
        pk = ("ps4", "ps6", "ps7")[k % 3]
        mm(V(pk, 0, 480), V("LY", p1=5), V("R", OFF + a, OFF + b, p1=5), True, False)
        mm(V(pk, 0, 480), V("ID8"), V("X0", a, b), False, True)
        tt(V("Y", OFF + a, OFF + b), V("X0", a, b), V(pk, 0, 480), ALU.min)

    def grant_constants():
        ts(V("PKU"), V("GON"), col(14), ALU.mult)
        ts(V("PKO"), V("GON"), col(13), ALU.mult)
        ts(V("PEN", 0, 64), V("IR", 0, 64), col(1), ALU.not_equal, -BIG, ALU.mult)
        ts(V("PEN", 64, 96), V("IX", 0, 32), col(1), ALU.is_le, BIG, ALU.mult)
        ts(V("PT", 32, 64), V("IX", 0, 32), -16.0, ALU.add, col(1), ALU.is_le)
        ts(V("PEN2"), V("PEN", 0, 32), 16.0, ALU.add)
        ts(V("GNN"), V("GON"), -1.0 / 32768.0, ALU.mult)
        ts(V("SEG"), V("IR", 0, 64), 0.5, ALU.is_lt, -4.0 * BIG, ALU.mult)
        ts(V("PEN", 96, 128), V("PT", 32, 64), BIG, ALU.mult)
        ts(V("JB"), V("IX", 0, 8), 16.0, ALU.mult, col(1), ALU.add)
        ts(V("KD", 0, 1), V("CODE", DEF, DEF + 1), col(15), ALU.mult, col(16), ALU.add)
        ts(V("DJ", 0, 2), V("JB", 0, 2), DMP + 0.25, ALU.add)
        tt(col(22), V("KD", 0, 1), V("CODE", DEF, DEF + 1), ALU.max)
        ts(V("JB"), V("JB"), float(NG), ALU.add)
        ts(V("EX16"), V("EXI"), OFF + 0.25, ALU.add)
        ts(V("KD"), V("IX", 0, 32), 0.0, ALU.mult, col(22), ALU.add)
        ts(V("P1"), V("IX", 0, 128), col(17), ALU.is_equal)
        ts(V("P2"), V("IX", 0, 128), col(18), ALU.is_equal)

    def wake_constants():
        ts(V("BE"), V("IX"), col(20), ALU.is_equal, col(19), ALU.mult)
        ts(V("BEF"), V("IX"), col(20), ALU.is_equal, col(19), ALU.mult)
        ts(V("BO"), V("IX"), col(21), ALU.is_equal, col(19), ALU.mult)
        ts(V("BF"), V("IX"), col(6), ALU.is_equal)

    masks, used = {}, set()
    for p in sorted([cores[rank ^ d] for d in range(1, N)], key=lambda c: len(topo.engines(core, c))):
        assert topo.may_write(core, p)
        es = [e for e in topo.engines(core, p) if e not in used][:4]
        used.update(es)
        masks[p] = sum(1 << e for e in es)
    n_arr = 4 * (N - 1)

    def send(t):
        def emit(e):
            trs = []
            for d in range(1, N):
                p = cores[rank ^ d]
                rid, pid, _ = topo.addr(p)
                a = 192 * t + NE * (d - 1)
                trs.append(RemoteDMATransfer(dst_ids=[DstId(rid=rid, pnc=pid)], dma_engine_mask=masks[p],
                                             remote_sem=T.sem["arr%d" % t], src=T["SND"][:, a:a + NE],
                                             dst=T["LAND"][:, a:a + NE]))
            e.remote_dma_fused(trs, local_sem=T.sem.sent)
            return None
        add("g", emit, [], [V("SND", 192 * t, 192 * t + 192)], kind="r")

    def refresh(tab, tmp, t, fill):
        for k in range(t, -1, -1):
            cp(V(tmp), X(V(tab), V("AL16", 4 * k, 4 * k + 2)))
            fill()
            cp(X(V(tab), V("AL16", 4 * k + 2, 4 * k + 4)), V(tmp))
            fill()

    for t in range(STEPS):
        std, sta = V("STD", 128 * t, 128 * t + 128), V("STA", 256 * t, 256 * t + 256)
        ct = "C"
        rows = list(range(KA[t], 16))

        def wake_row(rows=rows, std=std):
            if rows:
                r = rows.pop(0)
                cp(X(V("WE2" if r % 2 else "WE"), V("TB16", 8 * r, 8 * r + 8)), std)

        dq = DQ[t]
        for a, b in ((16 * dq, 256), (0, 16 * dq)) if NM2 else ((16 * dq, 16 * dq + 64), (0, 16 * dq), (16 * dq + 64, 256)):
            if NMP and b - a > 64:
                act(V("ps6", a, b), V("NA", a, b), AF.Copy)
                tt(V("NM", a, b), V("ND", a, b), V("ps6", a, b), ALU.max)
            else:
                tt(V("NM", a, b), V("ND", a, b), V("NA", a, b), ALU.max)
            bump[1] = 3.0
            ts(V("N16", a, b), V("NM", a, b), 0.25, ALU.add)
            bump[1] = 0.0
        if t + 1 < STEPS:
            iota(V("ND", 0, 256), [[0, 256]], 0, 0)
            iota(V("NA", 0, 256), [[0, 256]], 0, 0)
        cuts = [(q, min(q + 2, dq)) for q in range(0, dq, 2)] + [(q, min(q + 2, 16)) for q in range(dq, 16, 2)]
        for q, q2 in cuts:
            src = X(V("Y"), V("N16", 16 * q, 16 * q2))
            if q < dq:
                cp(V("G", 256 * q, 256 * q2), src)
            else:
                act(V("G", 256 * q, 256 * q2), src, AF.Copy)
        mm(V("ps1", 0, 16), V("IDN"), V("CST"), True, False)
        for q, q2 in cuts:
            scan(V("SC", 256 * q, 256 * q2), V("D0M", 0, 256 * (q2 - q)), V("G", 256 * q, 256 * q2), 0.0, ALU.mult,
                 ALU.max)
        order = sorted(range(16), key=lambda q: (q // 2 + 0.5 if q < dq else (q - dq) // 2, q))
        for n, q in enumerate(order):
            mm(V("ps0", 0, 256), V("BCO", 15 - q, 143 - q), V("G", 256 * q, 256 * q + 256), n == 0, n == 15)
        for q in range(16):
            mm(V("ps1", 0, 16), V("BAL", 15 - q, 143 - q), V("SC", 256 * q + 14, 256 * q + 256, 16), False, q == 15)
        ts(V("ps5", 384, 480), V("PL"), V("ps3", 0, 1), ALU.add, 256.5, ALU.is_gt)
        bump[0] = BA
        if t == 0:
            for k in range(4):
                ts(V("C", OFF + 768 * k, OFF + 768 * k + 768), V("C", OFF + 768 * k, OFF + 768 * k + 768), EMPTY,
                   ALU.bitwise_and)
        bump[0] = 0.0
        bump[1] = 6.0
        tt(V("REST"), V("AW"), V("ps5", 384, 480), ALU.mult)
        bump[1] = 0.0
        scan(V("Q"), V("D0S"), V("ps0", 0, 256), 0.0, ALU.mult, ALU.add)
        Sn, So = V("Q", 14, 256, 16), V("Q", 15, 256, 16)
        ts(S_(0), Sn, 0.0, ALU.min)
        tt(S_(5), Sn, So, ALU.not_equal)
        tt(S_(6), Sn, So, ALU.max)
        tt(S_(1), S_(0), V("ps1", 0, 16), ALU.max)
        ts(S_(4), V("ps1", 0, 16), 240.0 * KM - 8000.0, ALU.add)
        tt(S_(2), S_(1), So, ALU.subtract)
        tt(S_(8), S_(5), S_(6), ALU.mult)
        tt(S_(3), S_(2), V("J16"), ALU.max)
        tt(S_(7), Sn, S_(4), ALU.is_gt)
        ts(V("OB16"), S_(3), 0.25 - CB, ALU.add)
        tt(S_(9), S_(7), S_(8), ALU.mult)
        tt(V("H"), X(V(ct), V("OB16")), V("JT"), ALU.min)
        ts(V("WN"), S_(9), -1000.0, ALU.is_lt, -1.0, ALU.mult)
        trn(V("TT"), V("H"))
        tt(S_(10), V("WN"), So, ALU.mult)
        scan(V("WP"), V("CST"), V("WN"), 0.0, ALU.max, ALU.subtract)
        tt(S_(11), S_(10), S_(3), ALU.max)
        mm(V("ps3", 0, 1), V("TRI"), V("WP", 15, 16), True, True)
        tt(S_(12), V("WN"), Sn, ALU.mult)
        ts(V("BW16"), S_(11), 0.25 - CB, ALU.add)
        bump[1] = BT
        ts(V("TB16", 128, 160), X(V("TT"), V("LR16", 8, 10)), 0.25, ALU.add)
        bump[1] = BT2
        ts(V("TB16", 0, 128), X(V("TT"), V("LR16", 0, 8)), 0.25, ALU.add)
        ts(V("TB16", 160, 256), X(V("TT"), V("LR16", 10, 16)), 0.25, ALU.add)
        bump[1] = 0.0
        ts(V("OW16"), S_(10), 0.25 - CB, ALU.add)
        act(V("OWG"), X(V("CODE"), V("OW16")), AF.Identity, bias=0.0, scale=V("SCF", t, t + 1))
        act(V("GO_"), V("OWG"), AF.Identity, bias=col(16), scale=col(15))
        act(V("MPA"), X(V("SC"), V("LM16")), AF.Copy)
        mm(V("ps7", 0, 256), V("IDN"), V("MPA"), True, False)
        mm(V("ps7", 0, 256), V("IDN"), V("OWG"), False, True)
        act(V("MP"), V("ps7", 0, 256), AF.Copy)
        for r in range(16, 32):
            bump[0] = -0.6 * min(r - 16, KA[t])
            act(X(V("WO"), V("TB16", 8 * r, 8 * r + 8)), V("STA", 256 * t, 256 * t + 128), AF.Silu)
        for r in range(KA[t]):
            bump[0] = B2 - 0.6 * r
            act(X(V("WO2"), V("TB16", 8 * r, 8 * r + 8)), V("STA", 256 * t, 256 * t + 128), AF.Silu)
        bump[0] = 0.0
        if t == 0:
            grant_constants()
        ts(V("UL16"), S_(12), 0.25 - CB, ALU.add)
        ts(S_(13), V("WN"), BIG, ALU.mult, BIG, ALU.add)
        cp(V("K", 0, 32), V("KD"))
        tt(S_(14), S_(13), V("WP"), ALU.add)
        tt(V("GK"), X(V("CODE"), V("UL16")), V("GO_"), ALU.max)
        tt(S_(15), S_(14), V("JK"), ALU.min)
        ts(V("KO16"), S_(15), V("ps3", 0, 1), ALU.add, -0.75, ALU.add)
        cp(X(V("K"), V("KO16")), V("GK"))
        mm(V("ps4", 0, 128), V("IDN"), V("PEN"), True, False)
        mm(V("ps4", 0, 32), V("PKU"), V("K", 0, 32), False, False)
        mm(V("ps4", 32, 64), V("PKO"), V("K", 0, 32), False, False)
        mm(V("ps4", 64, 96), V("PKU"), V("K", 0, 32), False, False)
        mm(V("ps4", 96, 128), V("PKU"), V("K", 0, 32), False, True)
        cp(X(V("Y"), V("BW16")), V("MP"))
        scan(V("LW"), V("SEG"), V("ps4", 0, 64), 0.0, ALU.add, ALU.max)
        ts(V("L16"), V("LW", 15, 64, 16), 0.25 - 65.0, ALU.add)
        ts(V("EQ", 0, 32), V("ps4", 64, 96), V("LW", 15, 16), ALU.is_equal)
        ts(V("EQ", 32, 64), V("ps4", 96, 128), V("LW", 31, 32), ALU.is_equal)
        cp(V("CC"), X(V(ct), V("L16")))
        ts(V("FL"), X(V("Y"), V("L16", 0, 2)), col(23), ALU.mult, V("SCF", 8 + t, 9 + t), ALU.is_lt)
        tt(V("MN"), V("CC", 0, 32), V("CC", 32, 64), ALU.max)
        tt(V("CN"), V("CC", 0, 32), V("CC", 32, 64), ALU.min)
        mm(V("ps3", 0, 32), V("IDN"), V("PEN2"), True, False)
        mm(V("ps3", 0, 32), V("GON"), V("EQ", 0, 32), False, False)
        mm(V("ps3", 0, 32), V("GON"), V("EQ", 32, 64), False, False)
        mm(V("ps3", 0, 32), V("GON"), V("FL"), False, False)
        mm(V("ps3", 0, 32), V("GNN"), V("MN"), False, True)
        wake_row()
        scan(V("XS"), V("SEG", 0, 32), V("ps3", 0, 32), 0.0, ALU.add, ALU.max)
        ts(V("X4", 0, 2), V("XS", 15, 32, 16), BIG, ALU.mult, 0.25 - 65.0, ALU.add)
        for b in range(2):
            ts(V("AL16", 4 * t + b, 4 * t + 4, 2), V("LW", 15 + 16 * b, 64, 32), V("X4", b, b + 1), ALU.add,
               V("DJ", b, b + 1), ALU.min)
        refresh("Y", "RV", t, lambda: None)
        cp(V("SND", 192 * t, 192 * t + 192), X(V("Y"), V("EX16")))
        send(t)
        cp(X(V("C"), V("AL16", 4 * t, 4 * t + 2)), V("CN"))
        if t > 0:
            bump[0] = 4.0 if t + 1 == STEPS else 0.0
            cp(X(V("CF"), V("AL16", 4 * t, 4 * t + 2)), V("CN"))
            bump[0] = 0.0
        if t == 0:
            for k in range(1, STEPS):
                iota(V("STA", 256 * k, 256 * k + 256), [[0, 256]], int(STAMP[k]), 0)
                iota(V("STD", 128 * k, 128 * k + 128), [[0, 128]], int(STAMP[k]), 0)
            wake_constants()
        if t == 1:
            iota(V("FT"), [[1, YW]], -OFF, 0)
        if t + 1 == STEPS:
            bump[0] = BL
            for k in range(STEPS):
                cp(X(V("Y"), V("AL16", 4 * k + 2, 4 * k + 4)), V("NEG"))
            for a, b in ((0, 1440), (1440, NV)):
                ts(V("YO", a, b), V("Y", OFF + a, OFF + b), -1.0, ALU.max)
                dma("s", T.yx[:, a:b], V("YO", a, b), 2.5)
            bump[0] = BFT
            refresh("FT", "RF", t, lambda: None)
            dma("s", T.yf[:], V("FT", OFF, DEF, p0=0, p1=128, ps=16), 2.5)
            bump[0] = 0.0
            for q in range(16):
                mm(V("ps7", 0, 192), V("BF", 15 - q, 143 - q), V("CF", OFF + 192 * q, OFF + 192 * q + 192), q == 0, q == 15)
        while len(rows) > 3:
            wake_row()
        land = V("LAND", 192 * t, 192 * t + 192)
        add("v", lambda e, land=land: e.tensor_scalar(ap(V("IS")), ap(land), KM, 0.0, ALU.mult, ALU.min), [V("IS")], [],
            ext=("arr%d" % t, n_arr))
        for d in range(1, N):
            pm, a = V(("IDN", "P1", "P2")[d % 3]), NE * (d - 1)
            mm(V("ps6", a, a + NE), pm, V("IS", a, a + NE), True, t == 0)
            if t > 0:
                mm(V("ps6", a, a + NE), pm, V("IP", a, a + NE), False, True)
        for d in range(1, N):
            pm, a = V(("IDN", "P1", "P2")[d % 3]), NE * (d - 1)
            mm(V("ps4", 128 + a, 128 + a + NE), pm, V("IS", a, a + NE), True, False)
            mm(V("ps4", 128 + a, 128 + a + NE), pm, V("LAND", 192 * t + a, 192 * t + a + NE), False, True)
        if t + 1 < STEPS:
            tt(V("Y", IMP, DEF), V("CODE", IMP, DEF), V("ps4", 128, 320), ALU.max)
        wake_row()
        tt(V("IH"), V(ct, IMP, DEF), V("ps6", 0, 192), ALU.subtract)
        wake_row()
        trn(V("IT"), V("IH"))
        wake_row()
        for b in range(6):
            ts(V("TI16", b, 192, 6), V("IT", 32 * b, 32 * b + 32), V("JB", b, b + 1), ALU.min, 0.25, ALU.add)
        for r in range(16, 32):
            act(X(V("WO"), V("TI16", 6 * r, 6 * r + 6)), V("STA", 256 * t, 256 * t + 96), AF.Silu)
        for k in range(3):
            act(V("WOB", 512 * k, 512 * k + 512), V("WO", 512 * k, 512 * k + 512), AF.Copy)
        irows = list(range(16))

        def import_row(irows=irows, t=t):
            if irows:
                r = irows.pop(0)
                cp(X(V("WE2" if r % 2 and r < W2L else "WE"), V("TI16", 6 * r, 6 * r + 6)), V("STD", 128 * t, 128 * t + 96))

        if t + 1 < STEPS:
            ts(V("IP"), land, 0.0, ALU.is_ge, -BIG, ALU.mult, after=[V("IS")])
            refresh("Y", "RV", t, import_row)
        else:
            ts(V("YO", NV, 3072), V("ps4", 128, 320), -1.0, ALU.max)
            dma("s", T.yx[:, NV:3072], V("YO", NV, 3072), 2.5)
            ts(V("YCI"), V("ps7", 0, 192), 16.0, ALU.add)
            ts(V("YCI"), V("YCI"), EMPTY, ALU.bitwise_and)
            ts(V("YCF"), V("YCI"), -16.0, ALU.add)
            dma("s", T.yc[:], V("YCF"), 2.5)
        while irows:
            import_row()
        mm(V("ps2", 0, 96), V("ID8"), V("REST"), True, False)
        if KA[t]:
            for q in range(16):
                mm(V("ps2", 0, 96), V("BEF", 15 - q, 143 - q), V("WO2", 96 * q, 96 * q + 96), False, False)
        for q in range(16):
            mm(V("ps2", 0, 96), V("BE", 15 - q, 143 - q), V("WE2", 96 * q, 96 * q + 96), False, False)
        two = [("BO", "WOB"), ("BE", "WE")]
        for n, (sel, win) in enumerate(two[::-1] if EVEN_FIRST else two):
            for q in range(16):
                mm(V("ps2", 0, 96), V(sel, 15 - q, 143 - q), V(win, 96 * q, 96 * q + 96), False, n == 1 and q == 15)
        for k in range(CFK[t], CFK[t + 1]):
            bump[0] = 0.0
            cp(V("CF", OFF + 384 * k, OFF + 384 * k + 384), V("C", OFF + 384 * k, OFF + 384 * k + 384))
        if t + 1 < STEPS:
            ranks(t + 1)
            compaction(t + 1)
        else:
            ts(V("YWF"), V("ps2", 0, 96), 0.81 * STAMP[t], ALU.is_ge)
            dma("s", T.yw[:], V("YWF"), 2.5)

    n_ops = len(ops)
    succ = [[] for _ in ops]
    for i, o in enumerate(ops):
        for j in o[2] | o[6]:
            succ[j].append(i)

    def gap(j, i):
        if j in ops[i][2]:
            return ops[j][8] + SEM
        return ops[j][8] if ops[j][3] == "r" and ops[i][5] is not None else 0.0

    prio = [0.0] * n_ops
    for i in range(n_ops - 1, -1, -1):
        prio[i] = ops[i][7] + ops[i][10] + max([ops[i][8]] + [gap(i, k) + prio[k] for k in succ[i]])
    left = [len(o[2] | o[6]) for o in ops]
    ready = [0.0] * n_ops
    pend = {q: [] for q in eng}
    free = {q: 0.0 for q in eng}
    for i in range(n_ops):
        if not left[i]:
            pend[ops[i][0]].append(i)
    prio = [p + o[9] for p, o in zip(prio, ops)]
    seq = []
    while len(seq) < n_ops:
        now, q = min((max(free[q], min(ready[i] for i in pend[q])), q) for q in eng if pend[q])
        i = max((i for i in pend[q] if ready[i] <= now + LOOK), key=lambda i: (prio[i], -i))
        pend[q].remove(i)
        seq.append(i)
        free[q] = max(now, ready[i]) + ops[i][7]
        for k in succ[i]:
            ready[k] = max(ready[k], free[q] + gap(i, k))
            left[k] -= 1
            if not left[k]:
                pend[ops[k][0]].append(k)
    place = {j: i for i, j in enumerate(seq)}
    ops = [ops[j] for j in seq]
    for o in ops:
        o[2] = {place[j] for j in o[2]}

    last, tops = {}, []
    for i, o in enumerate(ops):
        if o[3] == "c":
            last[o[0]] = i
        top = {}
        for j in o[2]:
            if ops[j][3] == "c":
                top[ops[j][0]] = max(top.get(ops[j][0], -1), j)
        tops.append(top)
    seen = {}
    for i, o in enumerate(ops):
        for q, j in tops[i].items():
            if seen.get((o[0], q), -1) < j:
                seen[(o[0], q)] = j
                ops[j][4] = True
    for i in last.values():
        ops[i][4] = True
    cnt = {"v": 0, "a": 0, "t": 0, "g": 0}
    val, waited, seen = {}, {}, {}
    for i, o in enumerate(ops):
        if o[3] == "c" and o[4]:
            cnt[o[0]] += 1
            val[i] = ("q" + o[0], cnt[o[0]])
        elif o[3] == "d":
            val[i] = ("dm%d" % ndma[0], 16)
            ndma[0] += 1
    for i, o in enumerate(ops):
        e = eng[o[0]]
        need = {}
        for j in o[2]:
            if ops[j][3] == "d":
                need[val[j][0]] = 16
        for q, j in tops[i].items():
            if seen.get((o[0], q), -1) < j:
                seen[(o[0], q)] = j
                need[val[j][0]] = val[j][1]
        if o[5] is not None:
            need[o[5][0]] = o[5][1]
        for s in sorted(need):
            if waited.get((o[0], s), 0) < need[s]:
                e.wait_ge(T.sem[s], need[s])
                waited[(o[0], s)] = need[s]
        r = o[1](e)
        if i in val:
            r.then_inc(T.sem[val[i][0]], 16 if o[3] == "d" else 1)
    g.wait_ge(T.sem.sent, n_arr * STEPS)
    for q in cnt:
        g.sync.wait_ge(T.sem["q" + q], cnt[q])
    for k in range(ndma[0]):
        g.sync.wait_ge(T.sem["dm%d" % k], 16)
